import numpy as np
import ml_dtypes


def mxq(x, axis, fmt="e4m3"):
    dtype, down = {"e4m3": (ml_dtypes.float8_e4m3fn, 7), "e5m2": (ml_dtypes.float8_e5m2, 14)}[fmt]
    v = np.moveaxis(np.asarray(x, np.float32).astype(ml_dtypes.bfloat16).astype(np.float64), axis, -1)
    blocks = v.reshape(v.shape[:-1] + (-1, 32))
    amax = np.abs(blocks).max(-1, keepdims=True)
    byte = np.maximum(np.where(amax > 0, np.frexp(amax)[1] - 1 + 127, 0) - down, 1)
    scale = np.exp2(byte - 127.0)
    codes = (blocks / scale).astype(np.float32).astype(dtype).astype(np.float64)
    return np.moveaxis((codes * scale).reshape(v.shape), -1, axis)


WIDE = False


def mx_kscale(k, group=512):
    if not WIDE:
        return np.ones(k)
    levels = np.array([18, -18])
    if group != 512:
        return np.exp2(np.random.permutation(np.resize(levels, k // group))).repeat(group)
    if k % 512:
        return np.exp2(np.random.permutation(np.resize(levels, k // 32))).repeat(32)
    a = np.empty((k // 512, 16))
    for p in range(k // 512):
        a[p, :8] = np.random.permutation(np.resize(levels, 8))
        for g in range(8):
            far = levels[np.abs(levels - a[p, g]) >= 10]
            a[p, g + 8] = far[np.random.randint(len(far))]
    return np.exp2(a.ravel()).repeat(32)


def f64(x):
    return np.asarray(x).astype(np.float64)


def gelu(v):
    return 0.5 * v * (1.0 + np.tanh(0.7978845608028654 * (v + 0.044715 * v ** 3)))


G, D, I, N, J = 4, 128, 128, 512, 128


def setup_inputs():
    n = np.random.standard_normal
    s_d = mx_kscale(D, 0)
    s_i = mx_kscale(I, 0)
    return {
        "x": (n((G, D, I)) * s_d[:, None]).astype(np.float32),
        "w1": (n((D, N)) / np.sqrt(D) / s_d[:, None]).astype(np.float32),
        "ni1": (np.random.uniform(0.5, 2.0, (G, I, 1)) * s_i[:, None]).astype(np.float32),
        "ad1": ((np.random.uniform(size=(G, I, J)) < 0.1) * np.random.uniform(0.5, 1.0, (G, I, J)) / 3 / s_i[:, None]).astype(np.float32),
        "w2": (n((D, N)) / np.sqrt(D) / s_d[:, None]).astype(np.float32),
        "ni2": (np.random.uniform(0.5, 2.0, (G, I, 1)) * s_i[:, None]).astype(np.float32),
        "ad2": ((np.random.uniform(size=(G, I, J)) < 0.1) * np.random.uniform(0.5, 1.0, (G, I, J)) / 3 / s_i[:, None]).astype(np.float32),
    }


def reference(x, w1, ni1, ad1, w2, ni2, ad2):
    xq = mxq(f64(x), 1, "e4m3")
    w1q = mxq(f64(w1), 0, "e4m3")
    z1 = xq.transpose(0, 2, 1) @ w1q
    h1 = z1 * f64(ni1)
    w2q = mxq(f64(w2), 0, "e4m3")
    z2 = xq.transpose(0, 2, 1) @ w2q
    h2 = z2 * f64(ni2)
    ad1q = mxq(f64(ad1), 1, "e4m3")
    h1q = mxq(h1, 1, "e4m3")
    ad2q = mxq(f64(ad2), 1, "e4m3")
    h2q = mxq(h2, 1, "e4m3")
    y = (ad1q.transpose(0, 2, 1) @ h1q) + (ad2q.transpose(0, 2, 1) @ h2q)
    out_ = gelu(y)
    return out_

@@ -1,0 +1,193 @@
+from contextlib import ExitStack
+
+import concourse.mybir as mybir
+
+G, D, I, N, J = 4, 128, 128, 512, 128
+FLOPS = 2 * 2 * G * I * D * N + 2 * 2 * G * J * I * N
+
+F32 = mybir.dt.float32
+BF16 = mybir.dt.bfloat16
+I32 = mybir.dt.int32
+U8 = mybir.dt.uint8
+FP8X4 = mybir.dt.float8_e4m3fn_x4
+ACT = mybir.ActivationFunctionType
+ALU = mybir.AluOpType
+
+P = 128
+R = 32
+PACK = 4
+RELS = 2
+HALF = N // 2
+CHUNK = 128
+W2_VECTOR_COLS = 96
+H_VECTOR_COLS = 336
+
+
+def interleave(copy, dst, src, c0, c1):
+    copy(
+        out=dst[:, c0:c1, :].rearrange("p (c i) t -> p c t i", i=4),
+        in_=src[:, :, c0:c1].rearrange("p t (c i) -> p c t i", i=4),
+    )
+
+
+def tile_rows_gnn_rgcn_kernel(tc, x, w1, ni1, ad1, w2, ni2, ad2, out):
+    nc = tc.nc
+    ws, nis, ads = (w1, w2), (ni1, ni2), (ad1, ad2)
+
+    def rows(g):
+        return slice(R * g, R * (g + 1))
+
+    def queue(g):
+        return nc.sync if g < 2 else nc.scalar
+
+    def half_of(g, phase):
+        return (g // 2 + phase) % 2
+
+    def quantize(codes, scales, src):
+        nc.vector.quantize_mx(out=codes.bitcast(FP8X4), scales=scales, in_=src.rearrange("p c t -> p (c t)"))
+
+    with ExitStack() as ctx:
+        sb = ctx.enter_context(tc.tile_pool(name="sb", bufs=1))
+        ps = ctx.enter_context(tc.psum_pool(name="ps", bufs=1))
+        ctx.enter_context(tc.manual_schedule())
+
+        def sbuf(name, shape, dtype):
+            return sb.tile(shape, dtype, name=name, align_bytes=64)
+
+        bank = [[ps.tile([P, N], F32, name="bank%d_%d" % (g, ph)) for ph in range(2)] for g in range(G)]
+
+        w_raw = [sbuf("w_raw%d" % r, [P, PACK, HALF], F32) for r in range(RELS)]
+        w_bf = [sbuf("w_bf%d" % r, [P, HALF, PACK], BF16) for r in range(RELS)]
+        w_words = RELS * HALF
+        w_mx = [sbuf("w_mx%d" % ph, [P, w_words + w_words // 4], I32) for ph in range(2)]
+        x_raw = sbuf("x_raw", [P, PACK, I], F32)
+        x_bf = sbuf("x_bf", [P, I, PACK], BF16)
+        x_codes = sbuf("x_codes", [P, I], I32)
+        x_scales = sbuf("x_scales", [P, I], U8)
+        ad_raw = [sbuf("ad_raw%d" % r, [P, PACK, J], F32) for r in range(RELS)]
+        ad_bf = sbuf("ad_bf", [P, RELS * J, PACK], BF16)
+        ad_codes = sbuf("ad_codes", [P, RELS * J], I32)
+        ad_scales = sbuf("ad_scales", [P, RELS * J], U8)
+        ni_rows = sbuf("ni_rows", [P, R], F32)
+        ni_cols = sbuf("ni_cols", [P, R], F32)
+        warm_in = sbuf("warm_in", [P, 8], F32)
+        warm_out = sbuf("warm_out", [P, 8], F32)
+        h_node = [[sbuf("h_node%d_%d" % (g, ph), [P, RELS * HALF], BF16) for ph in range(2)] for g in range(G)]
+        h_rows = [sbuf("h_rows%d" % ph, [P, PACK, RELS * HALF], BF16) for ph in range(2)]
+        h_bf = [sbuf("h_bf%d" % ph, [P, RELS * HALF, PACK], BF16) for ph in range(2)]
+        h_codes = [sbuf("h_codes%d" % ph, [P, RELS * HALF], I32) for ph in range(2)]
+        h_scales = [sbuf("h_scales%d" % ph, [P, RELS * HALF], U8) for ph in range(2)]
+        y = [[sbuf("y%d_%d" % (g, ph), [P, HALF], F32) for ph in range(2)] for g in range(G)]
+
+        def w_scales(ph):
+            return w_mx[ph][:, w_words:].bitcast(U8)
+
+        nc.vector.memset(warm_in[:], 0.0)
+        nc.vector.memset(ni_rows[:], 0.0)
+        nc.vector.memset(w_mx[0][:, w_words:], 0)
+
+        for r in range(RELS):
+            for g in (0, 2, 1, 3):
+                h = half_of(g, 0)
+                queue(g).dma_start(
+                    out=w_raw[r][rows(g), :, :],
+                    in_=ws[r][:, h * HALF : (h + 1) * HALF].rearrange("(p t) n -> p t n", t=PACK),
+                )
+        nc.scalar.activation(out=warm_out[:], in_=warm_in[:], func=ACT.Gelu_apprx_tanh)
+        nc.sync.dma_start(out=x_raw[:], in_=x.rearrange("g (p t) i -> (g p) t i", t=PACK))
+        for r in range(RELS):
+            nc.sync.dma_start(
+                out=ni_rows[4 * r : P : 8, :], in_=nis[r].rearrange("g (b c) o -> b g (c o)", c=R)
+            )
+        for r in range(RELS):
+            nc.sync.dma_start(out=ad_raw[r][:], in_=ads[r].rearrange("g (p t) j -> (g p) t j", t=PACK))
+
+        interleave(nc.vector.tensor_copy, w_bf[0], w_raw[0], 0, HALF)
+        quantize(w_mx[0][:, 0:HALF], w_scales(0)[:, 0:HALF], w_bf[0][:])
+        interleave(nc.vector.tensor_copy, w_bf[1], w_raw[1], 0, W2_VECTOR_COLS)
+        interleave(nc.scalar.copy, w_bf[1], w_raw[1], W2_VECTOR_COLS, HALF)
+        quantize(w_mx[0][:, HALF:w_words], w_scales(0)[:, HALF:w_words], w_bf[1][:])
+        interleave(nc.scalar.copy, x_bf, x_raw, 0, I)
+        quantize(x_codes[:], x_scales[:], x_bf[:])
+        nc.sync.dma_start(out=w_mx[1][0:64, :], in_=w_mx[0][64:128, :])
+        nc.scalar.dma_start(out=w_mx[1][64:128, :], in_=w_mx[0][0:64, :])
+        nc.vector.transpose(out=ni_cols[:], in_=ni_rows[:])
+
+        def features(ph):
+            for c0 in range(0, w_words, CHUNK):
+                for g in range(G):
+                    nc.tensor.matmul_mx(
+                        out=bank[g][ph][:, c0 : c0 + CHUNK],
+                        lhsT=x_codes[rows(g), :].bitcast(FP8X4),
+                        lhsT_scale=x_scales[rows(g), :],
+                        rhs=w_mx[ph][rows(g), c0 : c0 + CHUNK].bitcast(FP8X4),
+                        rhs_scale=w_scales(ph)[rows(g), c0 : c0 + CHUNK],
+                        start=True,
+                        stop=True,
+                    )
+
+        def weigh_on_scalar(g, ph):
+            for r in range(RELS):
+                cols = slice(r * HALF, (r + 1) * HALF)
+                col = 8 * g + 4 * r
+                nc.scalar.activation(
+                    out=h_node[g][ph][:, cols], in_=bank[g][ph][:, cols], func=ACT.Copy, scale=ni_cols[:, col : col + 1]
+                )
+
+        def weigh_on_vector(g, ph):
+            nc.vector.tensor_tensor(
+                out=h_node[g][ph][:].rearrange("p (r n) -> p r n", r=RELS),
+                in0=bank[g][ph][:].rearrange("p (r n) -> p r n", r=RELS),
+                in1=ni_cols[:, 8 * g : 8 * g + 8 : 4].unsqueeze(2).to_broadcast([P, RELS, HALF]),
+                op=ALU.mult,
+            )
+
+        def gather_nodes(g, ph):
+            queue(g).dma_start(out=h_rows[ph][rows(g), :, :], in_=h_node[g][ph][:])
+
+        for ph in range(2):
+            features(ph)
+            for g in range(2):
+                weigh_on_scalar(g, ph)
+                weigh_on_vector(g + 2, ph)
+                gather_nodes(g, ph)
+                gather_nodes(g + 2, ph)
+
+        interleave(nc.scalar.copy, ad_bf[:, 0:J, :], ad_raw[0], 0, J)
+        interleave(nc.vector.tensor_copy, ad_bf[:, J : 2 * J, :], ad_raw[1], 0, J)
+        quantize(ad_codes[:], ad_scales[:], ad_bf[:])
+
+        def quantize_h(ph):
+            interleave(nc.vector.tensor_copy, h_bf[ph], h_rows[ph], 0, HALF)
+            interleave(nc.vector.tensor_copy, h_bf[ph], h_rows[ph], HALF, H_VECTOR_COLS)
+            interleave(nc.scalar.copy, h_bf[ph], h_rows[ph], H_VECTOR_COLS, RELS * HALF)
+            for r in range(RELS):
+                cols = slice(r * HALF, (r + 1) * HALF)
+                quantize(h_codes[ph][:, cols], h_scales[ph][:, cols], h_bf[ph][:, cols, :])
+
+        def edges(ph):
+            for c0 in range(0, HALF, CHUNK):
+                for r in range(RELS):
+                    cols = slice(r * HALF + c0, r * HALF + c0 + CHUNK)
+                    for g in range(G):
+                        nc.tensor.matmul_mx(
+                            out=bank[g][ph][:, c0 : c0 + CHUNK],
+                            lhsT=ad_codes[rows(g), r * J : (r + 1) * J].bitcast(FP8X4),
+                            lhsT_scale=ad_scales[rows(g), r * J : (r + 1) * J],
+                            rhs=h_codes[ph][rows(g), cols].bitcast(FP8X4),
+                            rhs_scale=h_scales[ph][rows(g), cols],
+                            start=(r == 0),
+                            stop=(r == RELS - 1),
+                        )
+
+        def finish(ph):
+            for g in range(G):
+                h = half_of(g, ph)
+                nc.scalar.activation(out=y[g][ph][:], in_=bank[g][ph][:, 0:HALF], func=ACT.Gelu_apprx_tanh)
+                nc.sync.dma_start(out=out[g, :, h * HALF : (h + 1) * HALF], in_=y[g][ph][:])
+
+        for ph in range(2):
+            quantize_h(ph)
+            edges(ph)
+        for ph in range(2):
+            finish(ph)

@@ -19,7 +19,7 @@ PACK = 4
 RELS = 2
 HALF = N // 2
 CHUNK = 128
-W2_VECTOR_COLS = 96
+W_VECTOR_COLS = 168
 H_VECTOR_COLS = 336
 
 
@@ -34,14 +34,11 @@ def tile_rows_gnn_rgcn_kernel(tc, x, w1, ni1, ad1, w2, ni2, ad2, out):
     nc = tc.nc
     ws, nis, ads = (w1, w2), (ni1, ni2), (ad1, ad2)
 
-    def rows(g):
-        return slice(R * g, R * (g + 1))
+    def rows(g, count=1):
+        return slice(R * g, R * (g + count))
 
     def queue(g):
         return nc.sync if g < 2 else nc.scalar
-
-    def half_of(g, phase):
-        return (g // 2 + phase) % 2
 
     def quantize(codes, scales, src):
         nc.vector.quantize_mx(out=codes.bitcast(FP8X4), scales=scales, in_=src.rearrange("p c t -> p (c t)"))
@@ -54,12 +51,11 @@ def tile_rows_gnn_rgcn_kernel(tc, x, w1, ni1, ad1, w2, ni2, ad2, out):
         def sbuf(name, shape, dtype):
             return sb.tile(shape, dtype, name=name, align_bytes=64)
 
-        bank = [[ps.tile([P, N], F32, name="bank%d_%d" % (g, ph)) for ph in range(2)] for g in range(G)]
+        bank = [[ps.tile([P, N], F32, name="bank%d_%d" % (g, b)) for b in range(2)] for g in range(G)]
 
-        w_raw = [sbuf("w_raw%d" % r, [P, PACK, HALF], F32) for r in range(RELS)]
-        w_bf = [sbuf("w_bf%d" % r, [P, HALF, PACK], BF16) for r in range(RELS)]
-        w_words = RELS * HALF
-        w_mx = [sbuf("w_mx%d" % ph, [P, w_words + w_words // 4], I32) for ph in range(2)]
+        w_raw = sbuf("w_raw", [P, PACK, HALF], F32)
+        w_bf = sbuf("w_bf", [P, HALF, PACK], BF16)
+        w_mx = [sbuf("w_mx%d" % s, [P, HALF + HALF // 4], I32) for s in range(G)]
         x_raw = sbuf("x_raw", [P, PACK, I], F32)
         x_bf = sbuf("x_bf", [P, I, PACK], BF16)
         x_codes = sbuf("x_codes", [P, I], I32)
@@ -72,27 +68,26 @@ def tile_rows_gnn_rgcn_kernel(tc, x, w1, ni1, ad1, w2, ni2, ad2, out):
         ni_cols = sbuf("ni_cols", [P, R], F32)
         warm_in = sbuf("warm_in", [P, 8], F32)
         warm_out = sbuf("warm_out", [P, 8], F32)
-        h_node = [[sbuf("h_node%d_%d" % (g, ph), [P, RELS * HALF], BF16) for ph in range(2)] for g in range(G)]
-        h_rows = [sbuf("h_rows%d" % ph, [P, PACK, RELS * HALF], BF16) for ph in range(2)]
-        h_bf = [sbuf("h_bf%d" % ph, [P, RELS * HALF, PACK], BF16) for ph in range(2)]
-        h_codes = [sbuf("h_codes%d" % ph, [P, RELS * HALF], I32) for ph in range(2)]
-        h_scales = [sbuf("h_scales%d" % ph, [P, RELS * HALF], U8) for ph in range(2)]
-        y = [[sbuf("y%d_%d" % (g, ph), [P, HALF], F32) for ph in range(2)] for g in range(G)]
+        widths = (HALF, CHUNK, CHUNK)
+        h_node = [[sbuf("h_node%d_%d" % (g, k), [P, RELS, wd], BF16) for k, wd in enumerate(widths)] for g in range(G)]
+        h_rows = [sbuf("h_rows%d" % k, [P, PACK, RELS * wd], BF16) for k, wd in enumerate(widths)]
+        h_bf = [sbuf("h_bf%d" % k, [P, RELS * wd, PACK], BF16) for k, wd in enumerate(widths)]
+        h_codes = [sbuf("h_codes%d" % k, [P, RELS * wd], I32) for k, wd in enumerate(widths)]
+        h_scales = [sbuf("h_scales%d" % k, [P, RELS * wd], U8) for k, wd in enumerate(widths)]
+        y = [[sbuf("y%d_%d" % (e, k), [P, 2, wd], F32) for k, wd in enumerate(widths)] for e in range(2)]
 
-        def w_scales(ph):
-            return w_mx[ph][:, w_words:].bitcast(U8)
+        def w_scales(s):
+            return w_mx[s][:, HALF:].bitcast(U8)
 
         nc.vector.memset(warm_in[:], 0.0)
         nc.vector.memset(ni_rows[:], 0.0)
-        nc.vector.memset(w_mx[0][:, w_words:], 0)
+        nc.vector.memset(w_mx[0][:, HALF:], 0)
 
-        for r in range(RELS):
-            for g in (0, 2, 1, 3):
-                h = half_of(g, 0)
-                queue(g).dma_start(
-                    out=w_raw[r][rows(g), :, :],
-                    in_=ws[r][:, h * HALF : (h + 1) * HALF].rearrange("(p t) n -> p t n", t=PACK),
-                )
+        for g in (0, 2, 1, 3):
+            queue(g).dma_start(
+                out=w_raw[rows(g), :, :],
+                in_=ws[g // 2][:, (g % 2) * HALF : (g % 2 + 1) * HALF].rearrange("(p t) n -> p t n", t=PACK),
+            )
         nc.scalar.activation(out=warm_out[:], in_=warm_in[:], func=ACT.Gelu_apprx_tanh)
         nc.sync.dma_start(out=x_raw[:], in_=x.rearrange("g (p t) i -> (g p) t i", t=PACK))
         for r in range(RELS):
@@ -102,92 +97,117 @@ def tile_rows_gnn_rgcn_kernel(tc, x, w1, ni1, ad1, w2, ni2, ad2, out):
         for r in range(RELS):
             nc.sync.dma_start(out=ad_raw[r][:], in_=ads[r].rearrange("g (p t) j -> (g p) t j", t=PACK))
 
-        interleave(nc.vector.tensor_copy, w_bf[0], w_raw[0], 0, HALF)
-        quantize(w_mx[0][:, 0:HALF], w_scales(0)[:, 0:HALF], w_bf[0][:])
-        interleave(nc.vector.tensor_copy, w_bf[1], w_raw[1], 0, W2_VECTOR_COLS)
-        interleave(nc.scalar.copy, w_bf[1], w_raw[1], W2_VECTOR_COLS, HALF)
-        quantize(w_mx[0][:, HALF:w_words], w_scales(0)[:, HALF:w_words], w_bf[1][:])
+        interleave(nc.vector.tensor_copy, w_bf, w_raw, 0, CHUNK)
+        interleave(nc.vector.tensor_copy, w_bf, w_raw, CHUNK, W_VECTOR_COLS)
+        interleave(nc.scalar.copy, w_bf, w_raw, W_VECTOR_COLS, HALF)
+        for c0 in (0, CHUNK):
+            quantize(w_mx[0][:, c0 : c0 + CHUNK], w_scales(0)[:, c0 : c0 + CHUNK], w_bf[:, c0 : c0 + CHUNK, :])
         interleave(nc.scalar.copy, x_bf, x_raw, 0, I)
         quantize(x_codes[:], x_scales[:], x_bf[:])
-        nc.sync.dma_start(out=w_mx[1][0:64, :], in_=w_mx[0][64:128, :])
-        nc.scalar.dma_start(out=w_mx[1][64:128, :], in_=w_mx[0][0:64, :])
-        nc.vector.transpose(out=ni_cols[:], in_=ni_rows[:])
 
-        def features(ph):
-            for c0 in range(0, w_words, CHUNK):
+        def hand_on(engine, shift, src, count):
+            engine.dma_start(out=w_mx[shift][rows((src + shift) % G, count), :], in_=w_mx[0][rows(src, count), :])
+
+        hand_on(nc.sync, 2, 2, 2)
+        hand_on(nc.sync, 2, 0, 2)
+        hand_on(nc.sync, 1, 0, 2)
+        hand_on(nc.scalar, 1, 2, 1)
+        hand_on(nc.sync, 1, 3, 1)
+        hand_on(nc.scalar, 3, 1, 2)
+        hand_on(nc.sync, 3, 0, 1)
+        hand_on(nc.scalar, 3, 3, 1)
+
+        nc.vector.transpose(out=ni_cols[:], in_=ni_rows[:])
+        interleave(nc.scalar.copy, ad_bf[:, 0:J, :], ad_raw[0], 0, J)
+        interleave(nc.vector.tensor_copy, ad_bf[:, J : 2 * J, :], ad_raw[1], 0, J)
+
+        def relation(g, shift):
+            return ((g - shift) % G) // 2
+
+        def features(shift):
+            for c0 in (0, CHUNK):
                 for g in range(G):
+                    col = relation(g, shift) * HALF + c0
                     nc.tensor.matmul_mx(
-                        out=bank[g][ph][:, c0 : c0 + CHUNK],
+                        out=bank[g][shift % 2][:, col : col + CHUNK],
                         lhsT=x_codes[rows(g), :].bitcast(FP8X4),
                         lhsT_scale=x_scales[rows(g), :],
-                        rhs=w_mx[ph][rows(g), c0 : c0 + CHUNK].bitcast(FP8X4),
-                        rhs_scale=w_scales(ph)[rows(g), c0 : c0 + CHUNK],
+                        rhs=w_mx[shift][rows(g), c0 : c0 + CHUNK].bitcast(FP8X4),
+                        rhs_scale=w_scales(shift)[rows(g), c0 : c0 + CHUNK],
                         start=True,
                         stop=True,
                     )
 
-        def weigh_on_scalar(g, ph):
-            for r in range(RELS):
-                cols = slice(r * HALF, (r + 1) * HALF)
-                col = 8 * g + 4 * r
-                nc.scalar.activation(
-                    out=h_node[g][ph][:, cols], in_=bank[g][ph][:, cols], func=ACT.Copy, scale=ni_cols[:, col : col + 1]
-                )
+        def weigh(g, r, dst, src):
+            col = ni_cols[:, 8 * g + 4 * r : 8 * g + 4 * r + 1]
+            if g < 2:
+                nc.scalar.activation(out=dst, in_=src, func=ACT.Copy, scale=col)
+            else:
+                nc.vector.tensor_scalar(out=dst, in0=src, scalar1=col, scalar2=None, op0=ALU.mult)
 
-        def weigh_on_vector(g, ph):
-            nc.vector.tensor_tensor(
-                out=h_node[g][ph][:].rearrange("p (r n) -> p r n", r=RELS),
-                in0=bank[g][ph][:].rearrange("p (r n) -> p r n", r=RELS),
-                in1=ni_cols[:, 8 * g : 8 * g + 8 : 4].unsqueeze(2).to_broadcast([P, RELS, HALF]),
-                op=ALU.mult,
-            )
+        def gather_nodes(g, k):
+            queue(g).dma_start(out=h_rows[k][rows(g), :, :], in_=h_node[g][k][:].rearrange("p r n -> p (r n)"))
 
-        def gather_nodes(g, ph):
-            queue(g).dma_start(out=h_rows[ph][rows(g), :, :], in_=h_node[g][ph][:])
+        def weigh_first_half(g, shift):
+            r = relation(g, shift)
+            weigh(g, r, h_node[g][0][:, r, :], bank[g][0][:, r * HALF : (r + 1) * HALF])
 
-        for ph in range(2):
-            features(ph)
-            for g in range(2):
-                weigh_on_scalar(g, ph)
-                weigh_on_vector(g + 2, ph)
-                gather_nodes(g, ph)
-                gather_nodes(g + 2, ph)
-
-        interleave(nc.scalar.copy, ad_bf[:, 0:J, :], ad_raw[0], 0, J)
-        interleave(nc.vector.tensor_copy, ad_bf[:, J : 2 * J, :], ad_raw[1], 0, J)
+        features(0)
+        for g in (0, 2, 1, 3):
+            weigh_first_half(g, 0)
         quantize(ad_codes[:], ad_scales[:], ad_bf[:])
+        features(2)
+        for g in (0, 2, 1, 3):
+            weigh_first_half(g, 2)
+            gather_nodes(g, 0)
 
-        def quantize_h(ph):
-            interleave(nc.vector.tensor_copy, h_bf[ph], h_rows[ph], 0, HALF)
-            interleave(nc.vector.tensor_copy, h_bf[ph], h_rows[ph], HALF, H_VECTOR_COLS)
-            interleave(nc.scalar.copy, h_bf[ph], h_rows[ph], H_VECTOR_COLS, RELS * HALF)
-            for r in range(RELS):
-                cols = slice(r * HALF, (r + 1) * HALF)
-                quantize(h_codes[ph][:, cols], h_scales[ph][:, cols], h_bf[ph][:, cols, :])
-
-        def edges(ph):
-            for c0 in range(0, HALF, CHUNK):
+        features(1)
+        features(3)
+        for k in (1, 2):
+            c0 = (k - 1) * CHUNK
+            for g in (0, 2, 1, 3):
                 for r in range(RELS):
-                    cols = slice(r * HALF + c0, r * HALF + c0 + CHUNK)
+                    weigh(g, r, h_node[g][k][:, r, :], bank[g][1][:, r * HALF + c0 : r * HALF + c0 + CHUNK])
+            for g in (0, 2, 1, 3):
+                gather_nodes(g, k)
+
+        def quantize_h(k):
+            wd = widths[k]
+            interleave(nc.vector.tensor_copy, h_bf[k], h_rows[k], 0, wd)
+            if k == 0:
+                interleave(nc.vector.tensor_copy, h_bf[k], h_rows[k], wd, H_VECTOR_COLS)
+                interleave(nc.scalar.copy, h_bf[k], h_rows[k], H_VECTOR_COLS, RELS * wd)
+            else:
+                interleave(nc.vector.tensor_copy, h_bf[k], h_rows[k], wd, RELS * wd)
+            for r in range(RELS):
+                cols = slice(r * wd, (r + 1) * wd)
+                quantize(h_codes[k][:, cols], h_scales[k][:, cols], h_bf[k][:, cols, :])
+
+        def edges(k):
+            wd = widths[k]
+            for c0 in range(0, wd, CHUNK):
+                for r in range(RELS):
+                    cols = slice(r * wd + c0, r * wd + c0 + CHUNK)
                     for g in range(G):
                         nc.tensor.matmul_mx(
-                            out=bank[g][ph][:, c0 : c0 + CHUNK],
+                            out=bank[g][k % 2][:, c0 : c0 + CHUNK],
                             lhsT=ad_codes[rows(g), r * J : (r + 1) * J].bitcast(FP8X4),
                             lhsT_scale=ad_scales[rows(g), r * J : (r + 1) * J],
-                            rhs=h_codes[ph][rows(g), cols].bitcast(FP8X4),
-                            rhs_scale=h_scales[ph][rows(g), cols],
+                            rhs=h_codes[k][rows(g), cols].bitcast(FP8X4),
+                            rhs_scale=h_scales[k][rows(g), cols],
                             start=(r == 0),
                             stop=(r == RELS - 1),
                         )
 
-        def finish(ph):
-            for g in range(G):
-                h = half_of(g, ph)
-                nc.scalar.activation(out=y[g][ph][:], in_=bank[g][ph][:, 0:HALF], func=ACT.Gelu_apprx_tanh)
-                nc.sync.dma_start(out=out[g, :, h * HALF : (h + 1) * HALF], in_=y[g][ph][:])
+        def finish(k):
+            wd = widths[k]
+            for e in range(2):
+                for g in (e, e + 2):
+                    nc.scalar.activation(out=y[e][k][:, g // 2, :], in_=bank[g][k % 2][:, 0:wd], func=ACT.Gelu_apprx_tanh)
+                c0 = e * HALF if k == 0 else (1 - e) * HALF + (k - 1) * CHUNK
+                nc.sync.dma_start(out=out[e:G:2, :, c0 : c0 + wd].rearrange("g j n -> j g n"), in_=y[e][k][:])
 
-        for ph in range(2):
-            quantize_h(ph)
-            edges(ph)
-        for ph in range(2):
-            finish(ph)
+        for k in range(len(widths)):
+            quantize_h(k)
+            edges(k)
+            finish(k)

@@ -20,7 +20,11 @@ RELS = 2
 HALF = N // 2
 CHUNK = 128
 W_VECTOR_COLS = 168
-H_VECTOR_COLS = 336
+GAP = P - R
+PIECES = PACK + 2
+SCALAR_BANKS = ((1, 0), (3, 0), (1, 1))
+EDGE = 16
+X_WORDS = EDGE + PIECES * P
 
 
 def interleave(copy, dst, src, c0, c1):
@@ -37,9 +41,6 @@ def tile_rows_gnn_rgcn_kernel(tc, x, w1, ni1, ad1, w2, ni2, ad2, out):
     def rows(g, count=1):
         return slice(R * g, R * (g + count))
 
-    def queue(g):
-        return nc.sync if g < 2 else nc.scalar
-
     def quantize(codes, scales, src):
         nc.vector.quantize_mx(out=codes.bitcast(FP8X4), scales=scales, in_=src.rearrange("p c t -> p (c t)"))
 
@@ -51,163 +52,190 @@ def tile_rows_gnn_rgcn_kernel(tc, x, w1, ni1, ad1, w2, ni2, ad2, out):
         def sbuf(name, shape, dtype):
             return sb.tile(shape, dtype, name=name, align_bytes=64)
 
-        bank = [[ps.tile([P, N], F32, name="bank%d_%d" % (g, b)) for b in range(2)] for g in range(G)]
+        bank = [[ps.tile([P, N], F32, name="bank%d_%d" % (c, k)) for k in range(2)] for c in range(G)]
 
         w_raw = sbuf("w_raw", [P, PACK, HALF], F32)
         w_bf = sbuf("w_bf", [P, HALF, PACK], BF16)
-        w_mx = [sbuf("w_mx%d" % s, [P, HALF + HALF // 4], I32) for s in range(G)]
+        w_codes = sbuf("w_codes", [P, HALF], I32)
+        w_scales = sbuf("w_scales", [P, HALF], U8)
         x_raw = sbuf("x_raw", [P, PACK, I], F32)
         x_bf = sbuf("x_bf", [P, I, PACK], BF16)
         x_codes = sbuf("x_codes", [P, I], I32)
         x_scales = sbuf("x_scales", [P, I], U8)
+        x_pad = [sbuf("x_pad%d" % s, [P, X_WORDS], I32) for s in range(G)]
         ad_raw = [sbuf("ad_raw%d" % r, [P, PACK, J], F32) for r in range(RELS)]
-        ad_bf = sbuf("ad_bf", [P, RELS * J, PACK], BF16)
-        ad_codes = sbuf("ad_codes", [P, RELS * J], I32)
-        ad_scales = sbuf("ad_scales", [P, RELS * J], U8)
-        ni_rows = sbuf("ni_rows", [P, R], F32)
-        ni_cols = sbuf("ni_cols", [P, R], F32)
+        ad_bf = [sbuf("ad_bf%d" % r, [P, J, PACK], BF16) for r in range(RELS)]
+        ad_codes = [sbuf("ad_codes%d" % r, [P, J], I32) for r in range(RELS)]
+        ad_scales = [sbuf("ad_scales%d" % r, [P, J], U8) for r in range(RELS)]
+        h_place = {ck: sbuf("h_place%d_%d" % ck, [P, PACK, CHUNK], BF16) for ck in SCALAR_BANKS}
+        ni_t = [sbuf("ni_t%d" % r, [P, PACK], F32) for r in range(RELS)]
         warm_in = sbuf("warm_in", [P, 8], F32)
         warm_out = sbuf("warm_out", [P, 8], F32)
-        widths = (HALF, CHUNK, CHUNK)
-        h_node = [[sbuf("h_node%d_%d" % (g, k), [P, RELS, wd], BF16) for k, wd in enumerate(widths)] for g in range(G)]
-        h_rows = [sbuf("h_rows%d" % k, [P, PACK, RELS * wd], BF16) for k, wd in enumerate(widths)]
-        h_bf = [sbuf("h_bf%d" % k, [P, RELS * wd, PACK], BF16) for k, wd in enumerate(widths)]
-        h_codes = [sbuf("h_codes%d" % k, [P, RELS * wd], I32) for k, wd in enumerate(widths)]
-        h_scales = [sbuf("h_scales%d" % k, [P, RELS * wd], U8) for k, wd in enumerate(widths)]
-        y = [[sbuf("y%d_%d" % (e, k), [P, 2, wd], F32) for k, wd in enumerate(widths)] for e in range(2)]
+        h_bf = [[sbuf("h_bf%d_%d" % (c, k), [P, CHUNK, PACK], BF16) for k in range(2)] for c in range(G)]
+        h_codes = [[sbuf("h_codes%d_%d" % (c, k), [P, CHUNK], I32) for k in range(2)] for c in range(G)]
+        h_scales = [[sbuf("h_scales%d_%d" % (c, k), [P, CHUNK], U8) for k in range(2)] for c in range(G)]
+        y = [[sbuf("y%d_%d" % (half, k), [P, G, CHUNK], F32) for k in range(2)] for half in range(2)]
 
-        def w_scales(s):
-            return w_mx[s][:, HALF:].bitcast(U8)
+        def pieces(s):
+            return x_pad[s][:, EDGE:].rearrange("p (a m) -> p a m", m=P)[:, :, 0:R]
+
+        def zero_gaps(s):
+            nc.vector.memset(x_pad[s][:, EDGE:].rearrange("p (a m) -> p a m", m=P)[:, 0 : PIECES - 1, R:P], 0)
+            last = EDGE + (PIECES - 1) * P + R
+            nc.vector.memset(x_pad[s][:, 0 : last + EDGE].rearrange("p (b e) -> p b e", e=EDGE)[:, 0 :: last // EDGE, :], 0)
 
         nc.vector.memset(warm_in[:], 0.0)
-        nc.vector.memset(ni_rows[:], 0.0)
-        nc.vector.memset(w_mx[0][:, HALF:], 0)
+        nc.vector.memset(x_scales[:], 0)
+        for s in (0, 2):
+            zero_gaps(s)
 
-        for g in (0, 2, 1, 3):
-            queue(g).dma_start(
-                out=w_raw[rows(g), :, :],
-                in_=ws[g // 2][:, (g % 2) * HALF : (g % 2 + 1) * HALF].rearrange("(p t) n -> p t n", t=PACK),
-            )
-        nc.scalar.activation(out=warm_out[:], in_=warm_in[:], func=ACT.Gelu_apprx_tanh)
         nc.sync.dma_start(out=x_raw[:], in_=x.rearrange("g (p t) i -> (g p) t i", t=PACK))
-        for r in range(RELS):
-            nc.sync.dma_start(
-                out=ni_rows[4 * r : P : 8, :], in_=nis[r].rearrange("g (b c) o -> b g (c o)", c=R)
+        for c in (2, 0, 3, 1):
+            (nc.sync if c < 2 else nc.scalar).dma_start(
+                out=w_raw[rows(c), :, :],
+                in_=ws[c % 2][:, (c // 2) * HALF : (c // 2 + 1) * HALF].rearrange("(p t) n -> p t n", t=PACK),
             )
-        for r in range(RELS):
+        def load_edges(r):
             nc.sync.dma_start(out=ad_raw[r][:], in_=ads[r].rearrange("g (p t) j -> (g p) t j", t=PACK))
+
+        load_edges(0)
+        nc.scalar.activation(out=warm_out[:], in_=warm_in[:], func=ACT.Gelu_apprx_tanh)
+
+        nc.vector.tensor_copy(
+            out=x_bf[:].rearrange("p (t m) j -> p t m j", t=PACK),
+            in_=x_raw[:].rearrange("p j (m t) -> p t m j", t=PACK),
+        )
+        quantize(x_codes[:], x_scales[:], x_bf[:])
+        nc.vector.tensor_copy(out=pieces(0)[:, 1 : 1 + PACK, :], in_=x_codes[:].rearrange("p (t m) -> p t m", t=PACK))
+        for twin in range(2):
+            nc.vector.tensor_copy(
+                out=pieces(0)[:, 0 :: PIECES - 1, :].rearrange("p a (e twin b) -> p a e twin b", e=2, twin=2)[:, :, :, twin, :],
+                in_=x_scales[:].bitcast(I32).rearrange("p (a e b) -> p a e b", a=2, e=2),
+            )
+
+        def hand_on(engine, shift, src, count):
+            engine.dma_start(out=pieces(shift)[rows((src + shift) % G, count)], in_=pieces(0)[rows(src, count)])
+
+        hand_on(nc.sync, 2, 2, 2)
+        hand_on(nc.scalar, 2, 0, 2)
+        hand_on(nc.sync, 1, 0, 2)
+        hand_on(nc.scalar, 1, 2, 1)
+        hand_on(nc.sync, 1, 3, 1)
+        hand_on(nc.scalar, 3, 3, 1)
+        hand_on(nc.sync, 3, 1, 2)
+        hand_on(nc.sync, 3, 0, 1)
+        for r in range(RELS):
+            nc.sync.dma_start(out=ni_t[r][:], in_=nis[r].rearrange("g (p t) o -> (g p) (t o)", t=PACK))
+        load_edges(1)
 
         interleave(nc.vector.tensor_copy, w_bf, w_raw, 0, CHUNK)
         interleave(nc.vector.tensor_copy, w_bf, w_raw, CHUNK, W_VECTOR_COLS)
         interleave(nc.scalar.copy, w_bf, w_raw, W_VECTOR_COLS, HALF)
         for c0 in (0, CHUNK):
-            quantize(w_mx[0][:, c0 : c0 + CHUNK], w_scales(0)[:, c0 : c0 + CHUNK], w_bf[:, c0 : c0 + CHUNK, :])
-        interleave(nc.scalar.copy, x_bf, x_raw, 0, I)
-        quantize(x_codes[:], x_scales[:], x_bf[:])
+            quantize(w_codes[:, c0 : c0 + CHUNK], w_scales[:, c0 : c0 + CHUNK], w_bf[:, c0 : c0 + CHUNK, :])
 
-        def hand_on(engine, shift, src, count):
-            engine.dma_start(out=w_mx[shift][rows((src + shift) % G, count), :], in_=w_mx[0][rows(src, count), :])
+        for s in (1, 3):
+            zero_gaps(s)
 
-        hand_on(nc.sync, 2, 2, 2)
-        hand_on(nc.sync, 2, 0, 2)
-        hand_on(nc.sync, 1, 0, 2)
-        hand_on(nc.scalar, 1, 2, 1)
-        hand_on(nc.sync, 1, 3, 1)
-        hand_on(nc.scalar, 3, 1, 2)
-        hand_on(nc.sync, 3, 0, 1)
-        hand_on(nc.scalar, 3, 3, 1)
-
-        nc.vector.transpose(out=ni_cols[:], in_=ni_rows[:])
-        interleave(nc.scalar.copy, ad_bf[:, 0:J, :], ad_raw[0], 0, J)
-        interleave(nc.vector.tensor_copy, ad_bf[:, J : 2 * J, :], ad_raw[1], 0, J)
-
-        def relation(g, shift):
-            return ((g - shift) % G) // 2
-
-        def features(shift):
-            for c0 in (0, CHUNK):
-                for g in range(G):
-                    col = relation(g, shift) * HALF + c0
+        def features(shift, k, first, last):
+            for t in range(PACK):
+                for c in range(G):
+                    g = (c - shift) % G
+                    word0 = EDGE + P * (1 + t) - R * g
+                    byte0 = 4 * (EDGE + P * (PIECES - 1) * (t // 2)) + 64 * (t % 2) - 64 * (g // 2)
                     nc.tensor.matmul_mx(
-                        out=bank[g][shift % 2][:, col : col + CHUNK],
-                        lhsT=x_codes[rows(g), :].bitcast(FP8X4),
-                        lhsT_scale=x_scales[rows(g), :],
-                        rhs=w_mx[shift][rows(g), c0 : c0 + CHUNK].bitcast(FP8X4),
-                        rhs_scale=w_scales(shift)[rows(g), c0 : c0 + CHUNK],
-                        start=True,
-                        stop=True,
+                        out=bank[c][k][:, t * CHUNK : (t + 1) * CHUNK],
+                        lhsT=x_pad[shift][rows(c), word0 : word0 + P].bitcast(FP8X4),
+                        lhsT_scale=x_pad[shift][:].bitcast(U8)[rows(c), byte0 : byte0 + P],
+                        rhs=w_codes[rows(c), k * CHUNK : (k + 1) * CHUNK].bitcast(FP8X4),
+                        rhs_scale=w_scales[rows(c), k * CHUNK : (k + 1) * CHUNK],
+                        start=(first and t == 0),
+                        stop=(last and t == PACK - 1),
                     )
 
-        def weigh(g, r, dst, src):
-            col = ni_cols[:, 8 * g + 4 * r : 8 * g + 4 * r + 1]
-            if g < 2:
-                nc.scalar.activation(out=dst, in_=src, func=ACT.Copy, scale=col)
-            else:
-                nc.vector.tensor_scalar(out=dst, in0=src, scalar1=col, scalar2=None, op0=ALU.mult)
+        for k in range(2):
+            features(0, k, True, False)
+        for k in range(2):
+            for shift in (2, 1, 3):
+                features(shift, k, False, shift == 3)
 
-        def gather_nodes(g, k):
-            queue(g).dma_start(out=h_rows[k][rows(g), :, :], in_=h_node[g][k][:].rearrange("p r n -> p (r n)"))
+        for r in range(RELS):
+            interleave(nc.scalar.copy, ad_bf[r], ad_raw[r], 0, J)
+            quantize(ad_codes[r][:], ad_scales[r][:], ad_bf[r][:])
 
-        def weigh_first_half(g, shift):
-            r = relation(g, shift)
-            weigh(g, r, h_node[g][0][:, r, :], bank[g][0][:, r * HALF : (r + 1) * HALF])
+        def weigh_places(c, k):
+            for t in range(PACK):
+                nc.scalar.activation(
+                    out=h_place[c, k][:, t, :],
+                    in_=bank[c][k][:, t * CHUNK : (t + 1) * CHUNK],
+                    func=ACT.Copy,
+                    scale=ni_t[c % 2][:, t : t + 1],
+                )
 
-        features(0)
-        for g in (0, 2, 1, 3):
-            weigh_first_half(g, 0)
-        quantize(ad_codes[:], ad_scales[:], ad_bf[:])
-        features(2)
-        for g in (0, 2, 1, 3):
-            weigh_first_half(g, 2)
-            gather_nodes(g, 0)
+        def join_places(c, k):
+            interleave(nc.vector.tensor_copy, h_bf[c][k], h_place[c, k], 0, CHUNK)
 
-        features(1)
-        features(3)
-        for k in (1, 2):
-            c0 = (k - 1) * CHUNK
-            for g in (0, 2, 1, 3):
-                for r in range(RELS):
-                    weigh(g, r, h_node[g][k][:, r, :], bank[g][1][:, r * HALF + c0 : r * HALF + c0 + CHUNK])
-            for g in (0, 2, 1, 3):
-                gather_nodes(g, k)
+        def weigh(c, k):
+            nc.vector.tensor_tensor(
+                out=h_bf[c][k][:],
+                in0=bank[c][k][:].rearrange("p (t n) -> p n t", t=PACK),
+                in1=ni_t[c % 2][:].unsqueeze(1).to_broadcast([P, CHUNK, PACK]),
+                op=ALU.mult,
+            )
 
-        def quantize_h(k):
-            wd = widths[k]
-            interleave(nc.vector.tensor_copy, h_bf[k], h_rows[k], 0, wd)
-            if k == 0:
-                interleave(nc.vector.tensor_copy, h_bf[k], h_rows[k], wd, H_VECTOR_COLS)
-                interleave(nc.scalar.copy, h_bf[k], h_rows[k], H_VECTOR_COLS, RELS * wd)
-            else:
-                interleave(nc.vector.tensor_copy, h_bf[k], h_rows[k], wd, RELS * wd)
+        def quantize_h(c, k):
+            quantize(h_codes[c][k][:], h_scales[c][k][:], h_bf[c][k][:])
+
+        def result(g, half, k):
+            slot = 2 * k + half
+            return bank[g][slot // 3][:, (slot % 3) * CHUNK : (slot % 3 + 1) * CHUNK]
+
+        def edges(half, k):
             for r in range(RELS):
-                cols = slice(r * wd, (r + 1) * wd)
-                quantize(h_codes[k][:, cols], h_scales[k][:, cols], h_bf[k][:, cols, :])
+                c = 2 * half + r
+                for g in range(G):
+                    nc.tensor.matmul_mx(
+                        out=result(g, half, k),
+                        lhsT=ad_codes[r][rows(g), :].bitcast(FP8X4),
+                        lhsT_scale=ad_scales[r][rows(g), :],
+                        rhs=h_codes[c][k][rows(g), :].bitcast(FP8X4),
+                        rhs_scale=h_scales[c][k][rows(g), :],
+                        start=(r == 0),
+                        stop=(r == RELS - 1),
+                    )
 
-        def edges(k):
-            wd = widths[k]
-            for c0 in range(0, wd, CHUNK):
-                for r in range(RELS):
-                    cols = slice(r * wd + c0, r * wd + c0 + CHUNK)
-                    for g in range(G):
-                        nc.tensor.matmul_mx(
-                            out=bank[g][k % 2][:, c0 : c0 + CHUNK],
-                            lhsT=ad_codes[rows(g), r * J : (r + 1) * J].bitcast(FP8X4),
-                            lhsT_scale=ad_scales[rows(g), r * J : (r + 1) * J],
-                            rhs=h_codes[k][rows(g), cols].bitcast(FP8X4),
-                            rhs_scale=h_scales[k][rows(g), cols],
-                            start=(r == 0),
-                            stop=(r == RELS - 1),
-                        )
+        def finish(half, k):
+            for g in range(G):
+                nc.scalar.activation(
+                    out=y[half][k][:, g, :], in_=result(g, half, k), func=ACT.Gelu_apprx_tanh
+                )
+            c0 = half * HALF + k * CHUNK
+            nc.sync.dma_start(out=out[:, :, c0 : c0 + CHUNK].rearrange("g j n -> j g n"), in_=y[half][k][:])
 
-        def finish(k):
-            wd = widths[k]
-            for e in range(2):
-                for g in (e, e + 2):
-                    nc.scalar.activation(out=y[e][k][:, g // 2, :], in_=bank[g][k % 2][:, 0:wd], func=ACT.Gelu_apprx_tanh)
-                c0 = e * HALF if k == 0 else (1 - e) * HALF + (k - 1) * CHUNK
-                nc.sync.dma_start(out=out[e:G:2, :, c0 : c0 + wd].rearrange("g j n -> j g n"), in_=y[e][k][:])
-
-        for k in range(len(widths)):
-            quantize_h(k)
-            edges(k)
-            finish(k)
+        weigh_places(1, 0)
+        weigh_places(3, 0)
+        weigh_places(1, 1)
+        weigh(0, 0)
+        weigh(2, 0)
+        quantize_h(0, 0)
+        join_places(1, 0)
+        quantize_h(2, 0)
+        quantize_h(1, 0)
+        edges(0, 0)
+        finish(0, 0)
+        join_places(3, 0)
+        weigh(0, 1)
+        quantize_h(3, 0)
+        edges(1, 0)
+        finish(1, 0)
+        join_places(1, 1)
+        quantize_h(0, 1)
+        weigh(2, 1)
+        quantize_h(1, 1)
+        edges(0, 1)
+        finish(0, 1)
+        weigh(3, 1)
+        quantize_h(2, 1)
+        quantize_h(3, 1)
+        edges(1, 1)
+        finish(1, 1)

@@ -21,10 +21,6 @@ HALF = N // 2
 CHUNK = 128
 W_VECTOR_COLS = 168
 GAP = P - R
-PIECES = PACK + 2
-SCALAR_BANKS = ((1, 0), (3, 0), (1, 1))
-EDGE = 16
-X_WORDS = EDGE + PIECES * P
 
 
 def interleave(copy, dst, src, c0, c1):
@@ -60,61 +56,68 @@ def tile_rows_gnn_rgcn_kernel(tc, x, w1, ni1, ad1, w2, ni2, ad2, out):
         w_scales = sbuf("w_scales", [P, HALF], U8)
         x_raw = sbuf("x_raw", [P, PACK, I], F32)
         x_bf = sbuf("x_bf", [P, I, PACK], BF16)
-        x_codes = sbuf("x_codes", [P, I], I32)
-        x_scales = sbuf("x_scales", [P, I], U8)
-        x_pad = [sbuf("x_pad%d" % s, [P, X_WORDS], I32) for s in range(G)]
+        x_mx = [sbuf("x_mx%d" % s, [P, I + I // 4], I32) for s in range(G)]
+        x_pad = [sbuf("x_pad%d" % s, [P, GAP + PACK * P], I32) for s in range(G)]
+        x_scales = [sbuf("x_scales%d" % s, [P, PACK, P], U8) for s in range(G)]
         ad_raw = [sbuf("ad_raw%d" % r, [P, PACK, J], F32) for r in range(RELS)]
         ad_bf = [sbuf("ad_bf%d" % r, [P, J, PACK], BF16) for r in range(RELS)]
         ad_codes = [sbuf("ad_codes%d" % r, [P, J], I32) for r in range(RELS)]
         ad_scales = [sbuf("ad_scales%d" % r, [P, J], U8) for r in range(RELS)]
-        h_place = {ck: sbuf("h_place%d_%d" % ck, [P, PACK, CHUNK], BF16) for ck in SCALAR_BANKS}
         ni_t = [sbuf("ni_t%d" % r, [P, PACK], F32) for r in range(RELS)]
         warm_in = sbuf("warm_in", [P, 8], F32)
         warm_out = sbuf("warm_out", [P, 8], F32)
+        h_place = [[sbuf("h_place%d_%d" % (half, k), [P, PACK, CHUNK], BF16) for k in range(2)] for half in range(2)]
         h_bf = [[sbuf("h_bf%d_%d" % (c, k), [P, CHUNK, PACK], BF16) for k in range(2)] for c in range(G)]
         h_codes = [[sbuf("h_codes%d_%d" % (c, k), [P, CHUNK], I32) for k in range(2)] for c in range(G)]
         h_scales = [[sbuf("h_scales%d_%d" % (c, k), [P, CHUNK], U8) for k in range(2)] for c in range(G)]
-        y = [[sbuf("y%d_%d" % (half, k), [P, G, CHUNK], F32) for k in range(2)] for half in range(2)]
-
-        def pieces(s):
-            return x_pad[s][:, EDGE:].rearrange("p (a m) -> p a m", m=P)[:, :, 0:R]
+        y_first = sbuf("y_first", [P, 2, G, CHUNK], F32)
+        y_third = sbuf("y_third", [P, G, CHUNK], F32)
+        y_last = [sbuf("y_last%d" % e, [P, 2, CHUNK], F32) for e in range(2)]
 
         def zero_gaps(s):
-            nc.vector.memset(x_pad[s][:, EDGE:].rearrange("p (a m) -> p a m", m=P)[:, 0 : PIECES - 1, R:P], 0)
-            last = EDGE + (PIECES - 1) * P + R
-            nc.vector.memset(x_pad[s][:, 0 : last + EDGE].rearrange("p (b e) -> p b e", e=EDGE)[:, 0 :: last // EDGE, :], 0)
+            nc.vector.memset(x_pad[s][:, 0:GAP], 0)
+            nc.vector.memset(x_pad[s][:, GAP:].rearrange("p (t m) -> p t m", m=P)[:, :, R:P], 0)
+
+        def spread(s):
+            nc.vector.tensor_copy(
+                out=x_pad[s][:, GAP:].rearrange("p (t m) -> p t m", m=P)[:, :, 0:R],
+                in_=x_mx[s][:, 0:I].rearrange("p (t m) -> p t m", m=R),
+            )
+            nc.vector.tensor_copy(
+                out=x_scales[s][:].bitcast(I32).rearrange("p t (g b) -> p t g b", g=G),
+                in_=x_mx[s][:, I:].rearrange("p (t b) -> p t b", t=PACK).unsqueeze(2).to_broadcast([P, PACK, G, R // 4]),
+            )
+
+        def load_edges(r):
+            nc.sync.dma_start(out=ad_raw[r][:], in_=ads[r].rearrange("g (p t) j -> (g p) t j", t=PACK))
 
         nc.vector.memset(warm_in[:], 0.0)
-        nc.vector.memset(x_scales[:], 0)
-        for s in (0, 2):
+        nc.vector.memset(x_mx[0][:, I:], 0)
+        for s in (0, 2, 1):
             zero_gaps(s)
 
-        nc.sync.dma_start(out=x_raw[:], in_=x.rearrange("g (p t) i -> (g p) t i", t=PACK))
-        for c in (2, 0, 3, 1):
+        x_rows = x.rearrange("g (p t) i -> (g p) t i", t=PACK)
+        nc.sync.dma_start(out=x_raw[:, 0:2, :], in_=x_rows[:, 0:2, :])
+        nc.scalar.dma_start(out=x_raw[:, 2:4, :], in_=x_rows[:, 2:4, :])
+        for c in (0, 2, 1, 3):
             (nc.sync if c < 2 else nc.scalar).dma_start(
                 out=w_raw[rows(c), :, :],
                 in_=ws[c % 2][:, (c // 2) * HALF : (c // 2 + 1) * HALF].rearrange("(p t) n -> p t n", t=PACK),
             )
-        def load_edges(r):
-            nc.sync.dma_start(out=ad_raw[r][:], in_=ads[r].rearrange("g (p t) j -> (g p) t j", t=PACK))
-
         load_edges(0)
         nc.scalar.activation(out=warm_out[:], in_=warm_in[:], func=ACT.Gelu_apprx_tanh)
 
-        nc.vector.tensor_copy(
-            out=x_bf[:].rearrange("p (t m) j -> p t m j", t=PACK),
-            in_=x_raw[:].rearrange("p j (m t) -> p t m j", t=PACK),
-        )
-        quantize(x_codes[:], x_scales[:], x_bf[:])
-        nc.vector.tensor_copy(out=pieces(0)[:, 1 : 1 + PACK, :], in_=x_codes[:].rearrange("p (t m) -> p t m", t=PACK))
-        for twin in range(2):
-            nc.vector.tensor_copy(
-                out=pieces(0)[:, 0 :: PIECES - 1, :].rearrange("p a (e twin b) -> p a e twin b", e=2, twin=2)[:, :, :, twin, :],
-                in_=x_scales[:].bitcast(I32).rearrange("p (a e b) -> p a e b", a=2, e=2),
+        for u, copy in enumerate((nc.vector.tensor_copy, nc.scalar.copy)):
+            copy(
+                out=x_bf[:].rearrange("p (t m) j -> p t m j", t=PACK)[:, 2 * u : 2 * u + 2],
+                in_=x_raw[:].rearrange("p j (m t) -> p t m j", t=PACK)[:, 2 * u : 2 * u + 2],
             )
+        for u in range(2):
+            cols = slice(u * I // 2, (u + 1) * I // 2)
+            quantize(x_mx[0][:, cols], x_mx[0][:, I:].bitcast(U8)[:, cols], x_bf[:, cols, :])
 
         def hand_on(engine, shift, src, count):
-            engine.dma_start(out=pieces(shift)[rows((src + shift) % G, count)], in_=pieces(0)[rows(src, count)])
+            engine.dma_start(out=x_mx[shift][rows((src + shift) % G, count), :], in_=x_mx[0][rows(src, count), :])
 
         hand_on(nc.sync, 2, 2, 2)
         hand_on(nc.scalar, 2, 0, 2)
@@ -128,74 +131,67 @@ def tile_rows_gnn_rgcn_kernel(tc, x, w1, ni1, ad1, w2, ni2, ad2, out):
             nc.sync.dma_start(out=ni_t[r][:], in_=nis[r].rearrange("g (p t) o -> (g p) (t o)", t=PACK))
         load_edges(1)
 
+        zero_gaps(3)
+        spread(0)
         interleave(nc.vector.tensor_copy, w_bf, w_raw, 0, CHUNK)
         interleave(nc.vector.tensor_copy, w_bf, w_raw, CHUNK, W_VECTOR_COLS)
         interleave(nc.scalar.copy, w_bf, w_raw, W_VECTOR_COLS, HALF)
         for c0 in (0, CHUNK):
             quantize(w_codes[:, c0 : c0 + CHUNK], w_scales[:, c0 : c0 + CHUNK], w_bf[:, c0 : c0 + CHUNK, :])
+        for s in (2, 1, 3):
+            spread(s)
 
-        for s in (1, 3):
-            zero_gaps(s)
-
-        def features(shift, k, first, last):
+        def features(shift, k):
             for t in range(PACK):
                 for c in range(G):
-                    g = (c - shift) % G
-                    word0 = EDGE + P * (1 + t) - R * g
-                    byte0 = 4 * (EDGE + P * (PIECES - 1) * (t // 2)) + 64 * (t % 2) - 64 * (g // 2)
+                    word0 = GAP + P * t - R * ((c - shift) % G)
                     nc.tensor.matmul_mx(
                         out=bank[c][k][:, t * CHUNK : (t + 1) * CHUNK],
                         lhsT=x_pad[shift][rows(c), word0 : word0 + P].bitcast(FP8X4),
-                        lhsT_scale=x_pad[shift][:].bitcast(U8)[rows(c), byte0 : byte0 + P],
+                        lhsT_scale=x_scales[shift][rows(c), t, :],
                         rhs=w_codes[rows(c), k * CHUNK : (k + 1) * CHUNK].bitcast(FP8X4),
                         rhs_scale=w_scales[rows(c), k * CHUNK : (k + 1) * CHUNK],
-                        start=(first and t == 0),
-                        stop=(last and t == PACK - 1),
+                        start=(shift == 0 and t == 0),
+                        stop=(shift == 3 and t == PACK - 1),
                     )
 
         for k in range(2):
-            features(0, k, True, False)
-        for k in range(2):
-            for shift in (2, 1, 3):
-                features(shift, k, False, shift == 3)
+            for shift in (0, 2, 1, 3):
+                features(shift, k)
 
-        for r in range(RELS):
-            interleave(nc.scalar.copy, ad_bf[r], ad_raw[r], 0, J)
-            quantize(ad_codes[r][:], ad_scales[r][:], ad_bf[r][:])
+        interleave(nc.scalar.copy, ad_bf[0], ad_raw[0], 0, J)
+        quantize(ad_codes[0][:], ad_scales[0][:], ad_bf[0][:])
 
-        def weigh_places(c, k):
+        def weigh_places(half, k):
             for t in range(PACK):
                 nc.scalar.activation(
-                    out=h_place[c, k][:, t, :],
-                    in_=bank[c][k][:, t * CHUNK : (t + 1) * CHUNK],
+                    out=h_place[half][k][:, t, :],
+                    in_=bank[2 * half + 1][k][:, t * CHUNK : (t + 1) * CHUNK],
                     func=ACT.Copy,
-                    scale=ni_t[c % 2][:, t : t + 1],
+                    scale=ni_t[1][:, t : t + 1],
                 )
 
-        def join_places(c, k):
-            interleave(nc.vector.tensor_copy, h_bf[c][k], h_place[c, k], 0, CHUNK)
+        def join_places(half, k):
+            interleave(nc.vector.tensor_copy, h_bf[2 * half + 1][k], h_place[half][k], 0, CHUNK)
 
-        def weigh(c, k):
+        def weigh(half, k):
             nc.vector.tensor_tensor(
-                out=h_bf[c][k][:],
-                in0=bank[c][k][:].rearrange("p (t n) -> p n t", t=PACK),
-                in1=ni_t[c % 2][:].unsqueeze(1).to_broadcast([P, CHUNK, PACK]),
+                out=h_bf[2 * half][k][:],
+                in0=bank[2 * half][k][:].rearrange("p (t n) -> p n t", t=PACK),
+                in1=ni_t[0][:].unsqueeze(1).to_broadcast([P, CHUNK, PACK]),
                 op=ALU.mult,
             )
 
-        def quantize_h(c, k):
+        def quantize_h(half, r, k):
+            c = 2 * half + r
             quantize(h_codes[c][k][:], h_scales[c][k][:], h_bf[c][k][:])
 
-        def result(g, half, k):
-            slot = 2 * k + half
-            return bank[g][slot // 3][:, (slot % 3) * CHUNK : (slot % 3 + 1) * CHUNK]
-
-        def edges(half, k):
+        def edges(half, k, b, col):
             for r in range(RELS):
                 c = 2 * half + r
                 for g in range(G):
                     nc.tensor.matmul_mx(
-                        out=result(g, half, k),
+                        out=bank[g][b][:, col : col + CHUNK],
                         lhsT=ad_codes[r][rows(g), :].bitcast(FP8X4),
                         lhsT_scale=ad_scales[r][rows(g), :],
                         rhs=h_codes[c][k][rows(g), :].bitcast(FP8X4),
@@ -204,38 +200,46 @@ def tile_rows_gnn_rgcn_kernel(tc, x, w1, ni1, ad1, w2, ni2, ad2, out):
                         stop=(r == RELS - 1),
                     )
 
-        def finish(half, k):
-            for g in range(G):
-                nc.scalar.activation(
-                    out=y[half][k][:, g, :], in_=result(g, half, k), func=ACT.Gelu_apprx_tanh
-                )
-            c0 = half * HALF + k * CHUNK
-            nc.sync.dma_start(out=out[:, :, c0 : c0 + CHUNK].rearrange("g j n -> j g n"), in_=y[half][k][:])
+        def gelu(dst, src):
+            nc.scalar.activation(out=dst, in_=src, func=ACT.Gelu_apprx_tanh)
 
-        weigh_places(1, 0)
-        weigh_places(3, 0)
-        weigh_places(1, 1)
+        def store(graphs, col, src):
+            nc.sync.dma_start(out=out[graphs, :, col : col + CHUNK].rearrange("g j n -> j g n"), in_=src)
+
+        for half in range(2):
+            weigh_places(half, 0)
+        interleave(nc.scalar.copy, ad_bf[1], ad_raw[1], 0, J)
+        for half in range(2):
+            weigh_places(half, 1)
         weigh(0, 0)
-        weigh(2, 0)
-        quantize_h(0, 0)
+        weigh(1, 0)
+        quantize_h(0, 0, 0)
+        join_places(0, 0)
+        quantize_h(1, 0, 0)
         join_places(1, 0)
-        quantize_h(2, 0)
-        quantize_h(1, 0)
-        edges(0, 0)
-        finish(0, 0)
-        join_places(3, 0)
+        quantize_h(0, 1, 0)
+        quantize(ad_codes[1][:], ad_scales[1][:], ad_bf[1][:])
+        edges(0, 0, 0, 0)
         weigh(0, 1)
-        quantize_h(3, 0)
-        edges(1, 0)
-        finish(1, 0)
+        quantize_h(1, 1, 0)
+        edges(1, 0, 0, CHUNK)
+        for g in range(G):
+            gelu(y_first[:, :, g, :], bank[g][0][:, 0:HALF].rearrange("p (h n) -> p h n", h=2))
+        for half in range(2):
+            store(slice(0, G), half * HALF, y_first[:, half])
+        join_places(0, 1)
+        quantize_h(0, 0, 1)
+        weigh(1, 1)
+        quantize_h(0, 1, 1)
+        edges(0, 1, 1, 0)
+        for g in range(G):
+            gelu(y_third[:, g, :], bank[g][1][:, 0:CHUNK])
+        store(slice(0, G), CHUNK, y_third[:])
         join_places(1, 1)
-        quantize_h(0, 1)
-        weigh(2, 1)
-        quantize_h(1, 1)
-        edges(0, 1)
-        finish(0, 1)
-        weigh(3, 1)
-        quantize_h(2, 1)
-        quantize_h(3, 1)
-        edges(1, 1)
-        finish(1, 1)
+        quantize_h(1, 0, 1)
+        quantize_h(1, 1, 1)
+        edges(1, 1, 0, HALF)
+        for e in range(2):
+            for g in (2 * e, 2 * e + 1):
+                gelu(y_last[e][:, g % 2, :], bank[g][0][:, HALF : HALF + CHUNK])
+            store(slice(2 * e, 2 * e + 2), HALF + CHUNK, y_last[e][:])

@@ -70,9 +70,12 @@ def tile_rows_gnn_rgcn_kernel(tc, x, w1, ni1, ad1, w2, ni2, ad2, out):
         h_bf = [[sbuf("h_bf%d_%d" % (c, k), [P, CHUNK, PACK], BF16) for k in range(2)] for c in range(G)]
         h_codes = [[sbuf("h_codes%d_%d" % (c, k), [P, CHUNK], I32) for k in range(2)] for c in range(G)]
         h_scales = [[sbuf("h_scales%d_%d" % (c, k), [P, CHUNK], U8) for k in range(2)] for c in range(G)]
-        y_first = sbuf("y_first", [P, 2, G, CHUNK], F32)
-        y_third = sbuf("y_third", [P, G, CHUNK], F32)
-        y_last = [sbuf("y_last%d" % e, [P, 2, CHUNK], F32) for e in range(2)]
+        y = {
+            (half, k, e): sbuf("y%d_%d_%d" % (half, k, e), [P, 2, CHUNK], F32)
+            for half in range(2)
+            for k in range(2)
+            for e in range(2)
+        }
 
         def zero_gaps(s):
             nc.vector.memset(x_pad[s][:, 0:GAP], 0)
@@ -200,17 +203,21 @@ def tile_rows_gnn_rgcn_kernel(tc, x, w1, ni1, ad1, w2, ni2, ad2, out):
                         stop=(r == RELS - 1),
                     )
 
-        def gelu(dst, src):
-            nc.scalar.activation(out=dst, in_=src, func=ACT.Gelu_apprx_tanh)
-
-        def store(graphs, col, src):
-            nc.sync.dma_start(out=out[graphs, :, col : col + CHUNK].rearrange("g j n -> j g n"), in_=src)
+        def finish(half, k, b, col):
+            n0 = half * HALF + k * CHUNK
+            for e in range(2):
+                for g in (2 * e, 2 * e + 1):
+                    nc.scalar.activation(
+                        out=y[half, k, e][:, g % 2, :], in_=bank[g][b][:, col : col + CHUNK], func=ACT.Gelu_apprx_tanh
+                    )
+                nc.sync.dma_start(
+                    out=out[2 * e : 2 * e + 2, :, n0 : n0 + CHUNK].rearrange("g j n -> j g n"), in_=y[half, k, e][:]
+                )
 
         for half in range(2):
             weigh_places(half, 0)
         interleave(nc.scalar.copy, ad_bf[1], ad_raw[1], 0, J)
-        for half in range(2):
-            weigh_places(half, 1)
+        weigh_places(0, 1)
         weigh(0, 0)
         weigh(1, 0)
         quantize_h(0, 0, 0)
@@ -220,26 +227,20 @@ def tile_rows_gnn_rgcn_kernel(tc, x, w1, ni1, ad1, w2, ni2, ad2, out):
         quantize_h(0, 1, 0)
         quantize(ad_codes[1][:], ad_scales[1][:], ad_bf[1][:])
         edges(0, 0, 0, 0)
+        finish(0, 0, 0, 0)
+        weigh_places(1, 1)
         weigh(0, 1)
         quantize_h(1, 1, 0)
         edges(1, 0, 0, CHUNK)
-        for g in range(G):
-            gelu(y_first[:, :, g, :], bank[g][0][:, 0:HALF].rearrange("p (h n) -> p h n", h=2))
-        for half in range(2):
-            store(slice(0, G), half * HALF, y_first[:, half])
+        finish(1, 0, 0, CHUNK)
         join_places(0, 1)
         quantize_h(0, 0, 1)
         weigh(1, 1)
         quantize_h(0, 1, 1)
         edges(0, 1, 1, 0)
-        for g in range(G):
-            gelu(y_third[:, g, :], bank[g][1][:, 0:CHUNK])
-        store(slice(0, G), CHUNK, y_third[:])
+        finish(0, 1, 1, 0)
         join_places(1, 1)
         quantize_h(1, 0, 1)
         quantize_h(1, 1, 1)
         edges(1, 1, 0, HALF)
-        for e in range(2):
-            for g in (2 * e, 2 * e + 1):
-                gelu(y_last[e][:, g % 2, :], bank[g][0][:, HALF : HALF + CHUNK])
-            store(slice(2 * e, 2 * e + 2), HALF + CHUNK, y_last[e][:])
+        finish(1, 1, 0, HALF)

@@ -19,7 +19,7 @@ PACK = 4
 RELS = 2
 HALF = N // 2
 CHUNK = 128
-W_VECTOR_COLS = 168
+W_VECTOR_COLS = 88
 GAP = P - R
 
 
@@ -50,10 +50,10 @@ def tile_rows_gnn_rgcn_kernel(tc, x, w1, ni1, ad1, w2, ni2, ad2, out):
 
         bank = [[ps.tile([P, N], F32, name="bank%d_%d" % (c, k)) for k in range(2)] for c in range(G)]
 
-        w_raw = sbuf("w_raw", [P, PACK, HALF], F32)
-        w_bf = sbuf("w_bf", [P, HALF, PACK], BF16)
-        w_codes = sbuf("w_codes", [P, HALF], I32)
-        w_scales = sbuf("w_scales", [P, HALF], U8)
+        w_raw = [sbuf("w_raw%d" % k, [P, PACK, CHUNK], F32) for k in range(2)]
+        w_bf = [sbuf("w_bf%d" % k, [P, CHUNK, PACK], BF16) for k in range(2)]
+        w_codes = [sbuf("w_codes%d" % k, [P, CHUNK], I32) for k in range(2)]
+        w_scales = [sbuf("w_scales%d" % k, [P, CHUNK], U8) for k in range(2)]
         x_raw = sbuf("x_raw", [P, PACK, I], F32)
         x_bf = sbuf("x_bf", [P, I, PACK], BF16)
         x_mx = [sbuf("x_mx%d" % s, [P, I + I // 4], I32) for s in range(G)]
@@ -102,12 +102,13 @@ def tile_rows_gnn_rgcn_kernel(tc, x, w1, ni1, ad1, w2, ni2, ad2, out):
         x_rows = x.rearrange("g (p t) i -> (g p) t i", t=PACK)
         nc.sync.dma_start(out=x_raw[:, 0:2, :], in_=x_rows[:, 0:2, :])
         nc.scalar.dma_start(out=x_raw[:, 2:4, :], in_=x_rows[:, 2:4, :])
-        for c in (0, 2, 1, 3):
-            (nc.sync if c < 2 else nc.scalar).dma_start(
-                out=w_raw[rows(c), :, :],
-                in_=ws[c % 2][:, (c // 2) * HALF : (c // 2 + 1) * HALF].rearrange("(p t) n -> p t n", t=PACK),
-            )
-        load_edges(0)
+        for k in range(2):
+            for c in (0, 2, 1, 3):
+                n0 = (c // 2) * HALF + k * CHUNK
+                (nc.sync if c < 2 or (c, k) == (3, 1) else nc.scalar).dma_start(
+                    out=w_raw[k][rows(c), :, :],
+                    in_=ws[c % 2][:, n0 : n0 + CHUNK].rearrange("(p t) n -> p t n", t=PACK),
+                )
         nc.scalar.activation(out=warm_out[:], in_=warm_in[:], func=ACT.Gelu_apprx_tanh)
 
         for u, copy in enumerate((nc.vector.tensor_copy, nc.scalar.copy)):
@@ -124,25 +125,27 @@ def tile_rows_gnn_rgcn_kernel(tc, x, w1, ni1, ad1, w2, ni2, ad2, out):
 
         hand_on(nc.sync, 2, 2, 2)
         hand_on(nc.scalar, 2, 0, 2)
+        spread(0)
+        interleave(nc.vector.tensor_copy, w_bf[0], w_raw[0], 0, W_VECTOR_COLS)
+        interleave(nc.scalar.copy, w_bf[0], w_raw[0], W_VECTOR_COLS, CHUNK)
+        quantize(w_codes[0][:], w_scales[0][:], w_bf[0][:])
         hand_on(nc.sync, 1, 0, 2)
         hand_on(nc.scalar, 1, 2, 1)
         hand_on(nc.sync, 1, 3, 1)
+        load_edges(0)
         hand_on(nc.scalar, 3, 3, 1)
         hand_on(nc.sync, 3, 1, 2)
         hand_on(nc.sync, 3, 0, 1)
-        for r in range(RELS):
-            nc.sync.dma_start(out=ni_t[r][:], in_=nis[r].rearrange("g (p t) o -> (g p) (t o)", t=PACK))
         load_edges(1)
 
+        interleave(nc.scalar.copy, w_bf[1], w_raw[1], 0, CHUNK)
+        for r in range(RELS):
+            nc.scalar.dma_start(out=ni_t[r][:], in_=nis[r].rearrange("g (p t) o -> (g p) (t o)", t=PACK))
         zero_gaps(3)
-        spread(0)
-        interleave(nc.vector.tensor_copy, w_bf, w_raw, 0, CHUNK)
-        interleave(nc.vector.tensor_copy, w_bf, w_raw, CHUNK, W_VECTOR_COLS)
-        interleave(nc.scalar.copy, w_bf, w_raw, W_VECTOR_COLS, HALF)
-        for c0 in (0, CHUNK):
-            quantize(w_codes[:, c0 : c0 + CHUNK], w_scales[:, c0 : c0 + CHUNK], w_bf[:, c0 : c0 + CHUNK, :])
-        for s in (2, 1, 3):
-            spread(s)
+        spread(2)
+        quantize(w_codes[1][:], w_scales[1][:], w_bf[1][:])
+        spread(1)
+        spread(3)
 
         def features(shift, k):
             for t in range(PACK):
@@ -152,8 +155,8 @@ def tile_rows_gnn_rgcn_kernel(tc, x, w1, ni1, ad1, w2, ni2, ad2, out):
                         out=bank[c][k][:, t * CHUNK : (t + 1) * CHUNK],
                         lhsT=x_pad[shift][rows(c), word0 : word0 + P].bitcast(FP8X4),
                         lhsT_scale=x_scales[shift][rows(c), t, :],
-                        rhs=w_codes[rows(c), k * CHUNK : (k + 1) * CHUNK].bitcast(FP8X4),
-                        rhs_scale=w_scales[rows(c), k * CHUNK : (k + 1) * CHUNK],
+                        rhs=w_codes[k][rows(c), :].bitcast(FP8X4),
+                        rhs_scale=w_scales[k][rows(c), :],
                         start=(shift == 0 and t == 0),
                         stop=(shift == 3 and t == PACK - 1),
                     )

@@ -91,61 +91,17 @@ def tile_rows_gnn_rgcn_kernel(tc, x, w1, ni1, ad1, w2, ni2, ad2, out):
                 in_=x_mx[s][:, I:].rearrange("p (t b) -> p t b", t=PACK).unsqueeze(2).to_broadcast([P, PACK, G, R // 4]),
             )
 
+        def load_w(engine, c, k):
+            n0 = (c // 2) * HALF + k * CHUNK
+            engine.dma_start(
+                out=w_raw[k][rows(c), :, :], in_=ws[c % 2][:, n0 : n0 + CHUNK].rearrange("(p t) n -> p t n", t=PACK)
+            )
+
         def load_edges(r):
             nc.sync.dma_start(out=ad_raw[r][:], in_=ads[r].rearrange("g (p t) j -> (g p) t j", t=PACK))
 
-        nc.vector.memset(warm_in[:], 0.0)
-        nc.vector.memset(x_mx[0][:, I:], 0)
-        for s in (0, 2, 1):
-            zero_gaps(s)
-
-        x_rows = x.rearrange("g (p t) i -> (g p) t i", t=PACK)
-        nc.sync.dma_start(out=x_raw[:, 0:2, :], in_=x_rows[:, 0:2, :])
-        nc.scalar.dma_start(out=x_raw[:, 2:4, :], in_=x_rows[:, 2:4, :])
-        for k in range(2):
-            for c in (0, 2, 1, 3):
-                n0 = (c // 2) * HALF + k * CHUNK
-                (nc.sync if c < 2 or (c, k) == (3, 1) else nc.scalar).dma_start(
-                    out=w_raw[k][rows(c), :, :],
-                    in_=ws[c % 2][:, n0 : n0 + CHUNK].rearrange("(p t) n -> p t n", t=PACK),
-                )
-        nc.scalar.activation(out=warm_out[:], in_=warm_in[:], func=ACT.Gelu_apprx_tanh)
-
-        for u, copy in enumerate((nc.vector.tensor_copy, nc.scalar.copy)):
-            copy(
-                out=x_bf[:].rearrange("p (t m) j -> p t m j", t=PACK)[:, 2 * u : 2 * u + 2],
-                in_=x_raw[:].rearrange("p j (m t) -> p t m j", t=PACK)[:, 2 * u : 2 * u + 2],
-            )
-        for u in range(2):
-            cols = slice(u * I // 2, (u + 1) * I // 2)
-            quantize(x_mx[0][:, cols], x_mx[0][:, I:].bitcast(U8)[:, cols], x_bf[:, cols, :])
-
         def hand_on(engine, shift, src, count):
             engine.dma_start(out=x_mx[shift][rows((src + shift) % G, count), :], in_=x_mx[0][rows(src, count), :])
-
-        hand_on(nc.sync, 2, 2, 2)
-        hand_on(nc.scalar, 2, 0, 2)
-        spread(0)
-        interleave(nc.vector.tensor_copy, w_bf[0], w_raw[0], 0, W_VECTOR_COLS)
-        interleave(nc.scalar.copy, w_bf[0], w_raw[0], W_VECTOR_COLS, CHUNK)
-        quantize(w_codes[0][:], w_scales[0][:], w_bf[0][:])
-        hand_on(nc.sync, 1, 0, 2)
-        hand_on(nc.scalar, 1, 2, 1)
-        hand_on(nc.sync, 1, 3, 1)
-        load_edges(0)
-        hand_on(nc.scalar, 3, 3, 1)
-        hand_on(nc.sync, 3, 1, 2)
-        hand_on(nc.sync, 3, 0, 1)
-        load_edges(1)
-
-        interleave(nc.scalar.copy, w_bf[1], w_raw[1], 0, CHUNK)
-        for r in range(RELS):
-            nc.scalar.dma_start(out=ni_t[r][:], in_=nis[r].rearrange("g (p t) o -> (g p) (t o)", t=PACK))
-        zero_gaps(3)
-        spread(2)
-        quantize(w_codes[1][:], w_scales[1][:], w_bf[1][:])
-        spread(1)
-        spread(3)
 
         def features(shift, k):
             for t in range(PACK):
@@ -161,12 +117,6 @@ def tile_rows_gnn_rgcn_kernel(tc, x, w1, ni1, ad1, w2, ni2, ad2, out):
                         stop=(shift == 3 and t == PACK - 1),
                     )
 
-        for k in range(2):
-            for shift in (0, 2, 1, 3):
-                features(shift, k)
-
-        interleave(nc.scalar.copy, ad_bf[0], ad_raw[0], 0, J)
-        quantize(ad_codes[0][:], ad_scales[0][:], ad_bf[0][:])
 
         def weigh_places(half, k):
             for t in range(PACK):
@@ -217,33 +167,91 @@ def tile_rows_gnn_rgcn_kernel(tc, x, w1, ni1, ad1, w2, ni2, ad2, out):
                     out=out[2 * e : 2 * e + 2, :, n0 : n0 + CHUNK].rearrange("g j n -> j g n"), in_=y[half, k, e][:]
                 )
 
-        for half in range(2):
-            weigh_places(half, 0)
-        interleave(nc.scalar.copy, ad_bf[1], ad_raw[1], 0, J)
+        nc.vector.memset(warm_in[:], 0.0)
+        nc.vector.memset(x_mx[0][:, I:], 0)
+        x_rows = x.rearrange("g (p t) i -> (g p) t i", t=PACK)
+        zero_gaps(0)
+        zero_gaps(2)
+        zero_gaps(1)
+        nc.sync.dma_start(out=x_raw[:, 0:2, :], in_=x_rows[:, 0:2, :])
+        nc.scalar.dma_start(out=x_raw[:, 2:4, :], in_=x_rows[:, 2:4, :])
+        load_w(nc.sync, 0, 0)
+        load_w(nc.scalar, 2, 0)
+        load_w(nc.sync, 1, 0)
+        load_w(nc.scalar, 3, 0)
+        load_w(nc.sync, 0, 1)
+        load_w(nc.scalar, 2, 1)
+        load_w(nc.sync, 1, 1)
+        nc.scalar.activation(out=warm_out[:], in_=warm_in[:], func=ACT.Gelu_apprx_tanh)
+        for u, copy in enumerate((nc.vector.tensor_copy, nc.scalar.copy)):
+            copy(
+                out=x_bf[:].rearrange("p (t m) j -> p t m j", t=PACK)[:, 2 * u : 2 * u + 2],
+                in_=x_raw[:].rearrange("p j (m t) -> p t m j", t=PACK)[:, 2 * u : 2 * u + 2],
+            )
+        load_w(nc.scalar, 3, 1)
+        for u in range(2):
+            cols = slice(u * I // 2, (u + 1) * I // 2)
+            quantize(x_mx[0][:, cols], x_mx[0][:, I:].bitcast(U8)[:, cols], x_bf[:, cols, :])
+        hand_on(nc.sync, 2, 2, 2)
+        hand_on(nc.scalar, 2, 0, 2)
+        spread(0)
+        interleave(nc.vector.tensor_copy, w_bf[0], w_raw[0], 0, W_VECTOR_COLS)
+        interleave(nc.scalar.copy, w_bf[0], w_raw[0], W_VECTOR_COLS, CHUNK)
+        quantize(w_codes[0][:], w_scales[0][:], w_bf[0][:])
+        hand_on(nc.sync, 1, 0, 2)
+        hand_on(nc.scalar, 1, 2, 1)
+        hand_on(nc.sync, 1, 3, 1)
+        hand_on(nc.scalar, 3, 3, 1)
+        hand_on(nc.sync, 3, 1, 2)
+        hand_on(nc.sync, 3, 0, 1)
+        load_edges(0)
+        load_edges(1)
+        for r in range(RELS):
+            nc.scalar.dma_start(out=ni_t[r][:], in_=nis[r].rearrange("g (p t) o -> (g p) (t o)", t=PACK))
+        zero_gaps(3)
+        spread(2)
+        interleave(nc.vector.tensor_copy, w_bf[1], w_raw[1], 0, W_VECTOR_COLS)
+        interleave(nc.scalar.copy, w_bf[1], w_raw[1], W_VECTOR_COLS, CHUNK)
+        spread(1)
+        quantize(w_codes[1][:], w_scales[1][:], w_bf[1][:])
+        spread(3)
+        features(0, 0)
+        features(2, 0)
+        features(1, 0)
+        features(3, 0)
+        features(0, 1)
+        features(2, 1)
+        features(1, 1)
+        features(3, 1)
+        weigh_places(0, 0)
+        interleave(nc.scalar.copy, ad_bf[0], ad_raw[0], 0, J)
+        weigh_places(1, 0)
         weigh_places(0, 1)
         weigh(0, 0)
         weigh(1, 0)
         quantize_h(0, 0, 0)
         join_places(0, 0)
-        quantize_h(1, 0, 0)
-        join_places(1, 0)
+        quantize(ad_codes[0][:], ad_scales[0][:], ad_bf[0][:])
+        interleave(nc.vector.tensor_copy, ad_bf[1], ad_raw[1], 0, J)
         quantize_h(0, 1, 0)
         quantize(ad_codes[1][:], ad_scales[1][:], ad_bf[1][:])
-        edges(0, 0, 0, 0)
-        finish(0, 0, 0, 0)
+        edges(0, 0, 0, 0 * CHUNK)
+        finish(0, 0, 0, 0 * CHUNK)
+        join_places(1, 0)
+        quantize_h(1, 0, 0)
         weigh_places(1, 1)
         weigh(0, 1)
         quantize_h(1, 1, 0)
-        edges(1, 0, 0, CHUNK)
-        finish(1, 0, 0, CHUNK)
+        edges(1, 0, 0, 1 * CHUNK)
+        finish(1, 0, 0, 1 * CHUNK)
         join_places(0, 1)
         quantize_h(0, 0, 1)
         weigh(1, 1)
         quantize_h(0, 1, 1)
-        edges(0, 1, 1, 0)
-        finish(0, 1, 1, 0)
+        edges(0, 1, 1, 0 * CHUNK)
+        finish(0, 1, 1, 0 * CHUNK)
         join_places(1, 1)
         quantize_h(1, 0, 1)
         quantize_h(1, 1, 1)
-        edges(1, 1, 0, HALF)
-        finish(1, 1, 0, HALF)
+        edges(1, 1, 0, 2 * CHUNK)
+        finish(1, 1, 0, 2 * CHUNK)

@@ -17,10 +17,11 @@ P = 128
 R = 32
 PACK = 4
 RELS = 2
-HALF = N // 2
 CHUNK = 128
-W_VECTOR_COLS = 88
+CHUNKS = 2
 GAP = P - R
+W_VECTOR_COLS = 88
+ROUNDS = (0, 2, 1, 3)
 
 
 def interleave(copy, dst, src, c0, c1):
@@ -34,8 +35,11 @@ def tile_rows_gnn_rgcn_kernel(tc, x, w1, ni1, ad1, w2, ni2, ad2, out):
     nc = tc.nc
     ws, nis, ads = (w1, w2), (ni1, ni2), (ad1, ad2)
 
-    def rows(g, count=1):
-        return slice(R * g, R * (g + count))
+    def rows(tile, count=1):
+        return slice(R * tile, R * (tile + count))
+
+    def first_column(half, k):
+        return k * 2 * CHUNK + half * CHUNK
 
     def quantize(codes, scales, src):
         nc.vector.quantize_mx(out=codes.bitcast(FP8X4), scales=scales, in_=src.rearrange("p c t -> p (c t)"))
@@ -48,12 +52,12 @@ def tile_rows_gnn_rgcn_kernel(tc, x, w1, ni1, ad1, w2, ni2, ad2, out):
         def sbuf(name, shape, dtype):
             return sb.tile(shape, dtype, name=name, align_bytes=64)
 
-        bank = [[ps.tile([P, N], F32, name="bank%d_%d" % (c, k)) for k in range(2)] for c in range(G)]
+        bank = [[ps.tile([P, N], F32, name="bank%d_%d" % (c, k)) for k in range(CHUNKS)] for c in range(G)]
 
-        w_raw = [sbuf("w_raw%d" % k, [P, PACK, CHUNK], F32) for k in range(2)]
-        w_bf = [sbuf("w_bf%d" % k, [P, CHUNK, PACK], BF16) for k in range(2)]
-        w_codes = [sbuf("w_codes%d" % k, [P, CHUNK], I32) for k in range(2)]
-        w_scales = [sbuf("w_scales%d" % k, [P, CHUNK], U8) for k in range(2)]
+        w_raw = [sbuf("w_raw%d" % k, [P, PACK, CHUNK], F32) for k in range(CHUNKS)]
+        w_bf = [sbuf("w_bf%d" % k, [P, CHUNK, PACK], BF16) for k in range(CHUNKS)]
+        w_codes = [sbuf("w_codes%d" % k, [P, CHUNK], I32) for k in range(CHUNKS)]
+        w_scales = [sbuf("w_scales%d" % k, [P, CHUNK], U8) for k in range(CHUNKS)]
         x_raw = sbuf("x_raw", [P, PACK, I], F32)
         x_bf = sbuf("x_bf", [P, I, PACK], BF16)
         x_mx = [sbuf("x_mx%d" % s, [P, I + I // 4], I32) for s in range(G)]
@@ -63,23 +67,35 @@ def tile_rows_gnn_rgcn_kernel(tc, x, w1, ni1, ad1, w2, ni2, ad2, out):
         ad_bf = [sbuf("ad_bf%d" % r, [P, J, PACK], BF16) for r in range(RELS)]
         ad_codes = [sbuf("ad_codes%d" % r, [P, J], I32) for r in range(RELS)]
         ad_scales = [sbuf("ad_scales%d" % r, [P, J], U8) for r in range(RELS)]
-        ni_t = [sbuf("ni_t%d" % r, [P, PACK], F32) for r in range(RELS)]
+        ni = [sbuf("ni%d" % r, [P, PACK], F32) for r in range(RELS)]
         warm_in = sbuf("warm_in", [P, 8], F32)
         warm_out = sbuf("warm_out", [P, 8], F32)
-        h_place = [[sbuf("h_place%d_%d" % (half, k), [P, PACK, CHUNK], BF16) for k in range(2)] for half in range(2)]
-        h_bf = [[sbuf("h_bf%d_%d" % (c, k), [P, CHUNK, PACK], BF16) for k in range(2)] for c in range(G)]
-        h_codes = [[sbuf("h_codes%d_%d" % (c, k), [P, CHUNK], I32) for k in range(2)] for c in range(G)]
-        h_scales = [[sbuf("h_scales%d_%d" % (c, k), [P, CHUNK], U8) for k in range(2)] for c in range(G)]
-        y = {
-            (half, k, e): sbuf("y%d_%d_%d" % (half, k, e), [P, 2, CHUNK], F32)
-            for half in range(2)
-            for k in range(2)
-            for e in range(2)
-        }
+        h_places = [[sbuf("h_places%d_%d" % (half, k), [P, PACK, CHUNK], BF16) for k in range(CHUNKS)] for half in range(2)]
+        h_bf = [[sbuf("h_bf%d_%d" % (c, k), [P, CHUNK, PACK], BF16) for k in range(CHUNKS)] for c in range(G)]
+        h_codes = [[sbuf("h_codes%d_%d" % (c, k), [P, CHUNK], I32) for k in range(CHUNKS)] for c in range(G)]
+        h_scales = [[sbuf("h_scales%d_%d" % (c, k), [P, CHUNK], U8) for k in range(CHUNKS)] for c in range(G)]
+        y_first = [sbuf("y_first%d" % g, [P, 2 * CHUNK], F32) for g in range(G)]
+        y_last = [[sbuf("y_last%d_%d" % (half, pair), [P, 2, CHUNK], F32) for pair in range(2)] for half in range(2)]
+
+        def load_w(queue, c, k):
+            n0 = first_column(c // RELS, k)
+            queue.dma_start(
+                out=w_raw[k][rows(c), :, :], in_=ws[c % RELS][:, n0 : n0 + CHUNK].rearrange("(p t) n -> p t n", t=PACK)
+            )
+
+        def round_w(k):
+            interleave(nc.vector.tensor_copy, w_bf[k], w_raw[k], 0, W_VECTOR_COLS)
+            interleave(nc.scalar.copy, w_bf[k], w_raw[k], W_VECTOR_COLS, CHUNK)
+
+        def quantize_w(k):
+            quantize(w_codes[k][:], w_scales[k][:], w_bf[k][:])
 
         def zero_gaps(s):
             nc.vector.memset(x_pad[s][:, 0:GAP], 0)
             nc.vector.memset(x_pad[s][:, GAP:].rearrange("p (t m) -> p t m", m=P)[:, :, R:P], 0)
+
+        def hand_on(queue, s, src, count):
+            queue.dma_start(out=x_mx[s][rows((src + s) % G, count), :], in_=x_mx[0][rows(src, count), :])
 
         def spread(s):
             nc.vector.tensor_copy(
@@ -91,56 +107,46 @@ def tile_rows_gnn_rgcn_kernel(tc, x, w1, ni1, ad1, w2, ni2, ad2, out):
                 in_=x_mx[s][:, I:].rearrange("p (t b) -> p t b", t=PACK).unsqueeze(2).to_broadcast([P, PACK, G, R // 4]),
             )
 
-        def load_w(engine, c, k):
-            n0 = (c // 2) * HALF + k * CHUNK
-            engine.dma_start(
-                out=w_raw[k][rows(c), :, :], in_=ws[c % 2][:, n0 : n0 + CHUNK].rearrange("(p t) n -> p t n", t=PACK)
-            )
-
-        def load_edges(r):
-            nc.sync.dma_start(out=ad_raw[r][:], in_=ads[r].rearrange("g (p t) j -> (g p) t j", t=PACK))
-
-        def hand_on(engine, shift, src, count):
-            engine.dma_start(out=x_mx[shift][rows((src + shift) % G, count), :], in_=x_mx[0][rows(src, count), :])
-
-        def features(shift, k):
+        def features(s, k):
             for t in range(PACK):
                 for c in range(G):
-                    word0 = GAP + P * t - R * ((c - shift) % G)
+                    word0 = GAP + P * t - R * ((c - s) % G)
                     nc.tensor.matmul_mx(
                         out=bank[c][k][:, t * CHUNK : (t + 1) * CHUNK],
-                        lhsT=x_pad[shift][rows(c), word0 : word0 + P].bitcast(FP8X4),
-                        lhsT_scale=x_scales[shift][rows(c), t, :],
+                        lhsT=x_pad[s][rows(c), word0 : word0 + P].bitcast(FP8X4),
+                        lhsT_scale=x_scales[s][rows(c), t, :],
                         rhs=w_codes[k][rows(c), :].bitcast(FP8X4),
                         rhs_scale=w_scales[k][rows(c), :],
-                        start=(shift == 0 and t == 0),
-                        stop=(shift == 3 and t == PACK - 1),
+                        start=(s == ROUNDS[0] and t == 0),
+                        stop=(s == ROUNDS[-1] and t == PACK - 1),
                     )
 
-
-        def weigh_places(half, k):
-            for t in range(PACK):
-                nc.scalar.activation(
-                    out=h_place[half][k][:, t, :],
-                    in_=bank[2 * half + 1][k][:, t * CHUNK : (t + 1) * CHUNK],
-                    func=ACT.Copy,
-                    scale=ni_t[1][:, t : t + 1],
-                )
-
-        def join_places(half, k):
-            interleave(nc.vector.tensor_copy, h_bf[2 * half + 1][k], h_place[half][k], 0, CHUNK)
-
-        def weigh(half, k):
+        def weigh_first(half, k):
             nc.vector.tensor_tensor(
                 out=h_bf[2 * half][k][:],
                 in0=bank[2 * half][k][:].rearrange("p (t n) -> p n t", t=PACK),
-                in1=ni_t[0][:].unsqueeze(1).to_broadcast([P, CHUNK, PACK]),
+                in1=ni[0][:].unsqueeze(1).to_broadcast([P, CHUNK, PACK]),
                 op=ALU.mult,
             )
+
+        def weigh_second(half, k):
+            for t in range(PACK):
+                nc.scalar.activation(
+                    out=h_places[half][k][:, t, :],
+                    in_=bank[2 * half + 1][k][:, t * CHUNK : (t + 1) * CHUNK],
+                    func=ACT.Copy,
+                    scale=ni[1][:, t : t + 1],
+                )
+
+        def join_second(half, k):
+            interleave(nc.vector.tensor_copy, h_bf[2 * half + 1][k], h_places[half][k], 0, CHUNK)
 
         def quantize_h(half, r, k):
             c = 2 * half + r
             quantize(h_codes[c][k][:], h_scales[c][k][:], h_bf[c][k][:])
+
+        def quantize_ad(r):
+            quantize(ad_codes[r][:], ad_scales[r][:], ad_bf[r][:])
 
         def edges(half, k, b, col):
             for r in range(RELS):
@@ -156,33 +162,35 @@ def tile_rows_gnn_rgcn_kernel(tc, x, w1, ni1, ad1, w2, ni2, ad2, out):
                         stop=(r == RELS - 1),
                     )
 
-        def finish(half, k, b, col):
-            n0 = half * HALF + k * CHUNK
-            for e in range(2):
-                for g in (2 * e, 2 * e + 1):
+        def finish_last(half, b, col):
+            n0 = first_column(half, 1)
+            for pair in range(2):
+                for e in range(2):
                     nc.scalar.activation(
-                        out=y[half, k, e][:, g % 2, :], in_=bank[g][b][:, col : col + CHUNK], func=ACT.Gelu_apprx_tanh
+                        out=y_last[half][pair][:, e, :],
+                        in_=bank[2 * pair + e][b][:, col : col + CHUNK],
+                        func=ACT.Gelu_apprx_tanh,
                     )
                 nc.sync.dma_start(
-                    out=out[2 * e : 2 * e + 2, :, n0 : n0 + CHUNK].rearrange("g j n -> j g n"), in_=y[half, k, e][:]
+                    out=out[2 * pair : 2 * pair + 2, :, n0 : n0 + CHUNK].rearrange("g j n -> j g n"), in_=y_last[half][pair][:]
                 )
 
         nc.vector.memset(warm_in[:], 0.0)
         nc.vector.memset(x_mx[0][:, I:], 0)
+        for s in ROUNDS[:3]:
+            zero_gaps(s)
+
         x_rows = x.rearrange("g (p t) i -> (g p) t i", t=PACK)
-        zero_gaps(0)
-        zero_gaps(2)
-        zero_gaps(1)
         nc.sync.dma_start(out=x_raw[:, 0:2, :], in_=x_rows[:, 0:2, :])
         nc.scalar.dma_start(out=x_raw[:, 2:4, :], in_=x_rows[:, 2:4, :])
-        load_w(nc.sync, 0, 0)
-        load_w(nc.scalar, 2, 0)
-        load_w(nc.sync, 1, 0)
-        load_w(nc.scalar, 3, 0)
-        load_w(nc.sync, 0, 1)
-        load_w(nc.scalar, 2, 1)
-        load_w(nc.sync, 1, 1)
+        for k in range(CHUNKS):
+            load_w(nc.sync, 0, k)
+            load_w(nc.scalar, 2, k)
+            load_w(nc.sync, 1, k)
+            if k == 0:
+                load_w(nc.scalar, 3, k)
         nc.scalar.activation(out=warm_out[:], in_=warm_in[:], func=ACT.Gelu_apprx_tanh)
+
         for u, copy in enumerate((nc.vector.tensor_copy, nc.scalar.copy)):
             copy(
                 out=x_bf[:].rearrange("p (t m) j -> p t m j", t=PACK)[:, 2 * u : 2 * u + 2],
@@ -192,66 +200,64 @@ def tile_rows_gnn_rgcn_kernel(tc, x, w1, ni1, ad1, w2, ni2, ad2, out):
         for u in range(2):
             cols = slice(u * I // 2, (u + 1) * I // 2)
             quantize(x_mx[0][:, cols], x_mx[0][:, I:].bitcast(U8)[:, cols], x_bf[:, cols, :])
+
         hand_on(nc.sync, 2, 2, 2)
         hand_on(nc.scalar, 2, 0, 2)
         spread(0)
-        interleave(nc.vector.tensor_copy, w_bf[0], w_raw[0], 0, W_VECTOR_COLS)
-        interleave(nc.scalar.copy, w_bf[0], w_raw[0], W_VECTOR_COLS, CHUNK)
-        quantize(w_codes[0][:], w_scales[0][:], w_bf[0][:])
+        round_w(0)
+        quantize_w(0)
         hand_on(nc.sync, 1, 0, 2)
         hand_on(nc.scalar, 1, 2, 1)
         hand_on(nc.sync, 1, 3, 1)
         hand_on(nc.scalar, 3, 3, 1)
         hand_on(nc.sync, 3, 1, 2)
         hand_on(nc.sync, 3, 0, 1)
-        load_edges(0)
-        load_edges(1)
         for r in range(RELS):
-            nc.scalar.dma_start(out=ni_t[r][:], in_=nis[r].rearrange("g (p t) o -> (g p) (t o)", t=PACK))
+            nc.sync.dma_start(out=ni[r][:], in_=nis[r].rearrange("g (p t) o -> (g p) (t o)", t=PACK))
+        for r in range(RELS):
+            nc.sync.dma_start(out=ad_raw[r][:], in_=ads[r].rearrange("g (p t) j -> (g p) t j", t=PACK))
+
         zero_gaps(3)
         spread(2)
-        interleave(nc.vector.tensor_copy, w_bf[1], w_raw[1], 0, W_VECTOR_COLS)
-        interleave(nc.scalar.copy, w_bf[1], w_raw[1], W_VECTOR_COLS, CHUNK)
+        round_w(1)
         spread(1)
-        quantize(w_codes[1][:], w_scales[1][:], w_bf[1][:])
+        quantize_w(1)
         spread(3)
-        features(0, 0)
-        features(2, 0)
-        features(1, 0)
-        features(3, 0)
-        features(0, 1)
-        features(2, 1)
-        features(1, 1)
-        features(3, 1)
-        weigh_places(0, 0)
+        for k in range(CHUNKS):
+            for s in ROUNDS:
+                features(s, k)
+
+        for half in range(2):
+            weigh_second(half, 0)
         interleave(nc.scalar.copy, ad_bf[0], ad_raw[0], 0, J)
-        weigh_places(1, 0)
-        weigh_places(0, 1)
-        weigh(0, 0)
-        weigh(1, 0)
-        quantize_h(0, 0, 0)
-        join_places(0, 0)
-        quantize(ad_codes[0][:], ad_scales[0][:], ad_bf[0][:])
+        for half in range(2):
+            weigh_second(half, 1)
+
+        for half in range(2):
+            weigh_first(half, 0)
+        for half in range(2):
+            quantize_h(half, 0, 0)
+            join_second(half, 0)
         interleave(nc.vector.tensor_copy, ad_bf[1], ad_raw[1], 0, J)
-        quantize_h(0, 1, 0)
-        quantize(ad_codes[1][:], ad_scales[1][:], ad_bf[1][:])
-        edges(0, 0, 0, 0 * CHUNK)
-        finish(0, 0, 0, 0 * CHUNK)
-        join_places(1, 0)
-        quantize_h(1, 0, 0)
-        weigh_places(1, 1)
-        weigh(0, 1)
-        quantize_h(1, 1, 0)
-        edges(1, 0, 0, 1 * CHUNK)
-        finish(1, 0, 0, 1 * CHUNK)
-        join_places(0, 1)
+        for half in range(2):
+            quantize_h(half, 1, 0)
+            quantize_ad(half)
+
+        for half in range(2):
+            edges(half, 0, 0, half * CHUNK)
+        for g in range(G):
+            nc.scalar.activation(out=y_first[g][:], in_=bank[g][0][:, 0 : 2 * CHUNK], func=ACT.Gelu_apprx_tanh)
+            nc.sync.dma_start(out=out[g, :, 0 : 2 * CHUNK], in_=y_first[g][:])
+
+        weigh_first(0, 1)
+        join_second(0, 1)
         quantize_h(0, 0, 1)
-        weigh(1, 1)
+        weigh_first(1, 1)
         quantize_h(0, 1, 1)
-        edges(0, 1, 1, 0 * CHUNK)
-        finish(0, 1, 1, 0 * CHUNK)
-        join_places(1, 1)
-        quantize_h(1, 0, 1)
-        quantize_h(1, 1, 1)
+        edges(0, 1, 1, 0)
+        finish_last(0, 1, 0)
+        join_second(1, 1)
+        for r in range(RELS):
+            quantize_h(1, r, 1)
         edges(1, 1, 0, 2 * CHUNK)
-        finish(1, 1, 0, 2 * CHUNK)
+        finish_last(1, 0, 2 * CHUNK)

@@ -193,8 +193,8 @@ def tile_rows_gnn_rgcn_kernel(tc, x, w1, ni1, ad1, w2, ni2, ad2, out):
 
         for u, copy in enumerate((nc.vector.tensor_copy, nc.scalar.copy)):
             copy(
-                out=x_bf[:].rearrange("p (t m) j -> p t m j", t=PACK)[:, 2 * u : 2 * u + 2],
-                in_=x_raw[:].rearrange("p j (m t) -> p t m j", t=PACK)[:, 2 * u : 2 * u + 2],
+                out=x_bf[:].rearrange("p (t m) j -> p m t j", t=PACK)[:, :, 2 * u : 2 * u + 2],
+                in_=x_raw[:].rearrange("p j (m t) -> p m t j", t=PACK)[:, :, 2 * u : 2 * u + 2],
             )
         load_w(nc.scalar, 3, 1)
         for u in range(2):

@@ -75,7 +75,7 @@ def tile_rows_gnn_rgcn_kernel(tc, x, w1, ni1, ad1, w2, ni2, ad2, out):
         h_codes = [[sbuf("h_codes%d_%d" % (c, k), [P, CHUNK], I32) for k in range(CHUNKS)] for c in range(G)]
         h_scales = [[sbuf("h_scales%d_%d" % (c, k), [P, CHUNK], U8) for k in range(CHUNKS)] for c in range(G)]
         y_first = [sbuf("y_first%d" % g, [P, 2 * CHUNK], F32) for g in range(G)]
-        y_last = [[sbuf("y_last%d_%d" % (half, pair), [P, 2, CHUNK], F32) for pair in range(2)] for half in range(2)]
+        y_last = [sbuf("y_last%d" % half, [P, G, CHUNK], F32) for half in range(2)]
 
         def load_w(queue, c, k):
             n0 = first_column(c // RELS, k)
@@ -162,17 +162,16 @@ def tile_rows_gnn_rgcn_kernel(tc, x, w1, ni1, ad1, w2, ni2, ad2, out):
                         stop=(r == RELS - 1),
                     )
 
-        def finish_last(half, b, col):
+        def finish_last(half, b, col, count):
             n0 = first_column(half, 1)
-            for pair in range(2):
-                for e in range(2):
+            for g0 in range(0, G, count):
+                for g in range(g0, g0 + count):
                     nc.scalar.activation(
-                        out=y_last[half][pair][:, e, :],
-                        in_=bank[2 * pair + e][b][:, col : col + CHUNK],
-                        func=ACT.Gelu_apprx_tanh,
+                        out=y_last[half][:, g, :], in_=bank[g][b][:, col : col + CHUNK], func=ACT.Gelu_apprx_tanh
                     )
                 nc.sync.dma_start(
-                    out=out[2 * pair : 2 * pair + 2, :, n0 : n0 + CHUNK].rearrange("g j n -> j g n"), in_=y_last[half][pair][:]
+                    out=out[g0 : g0 + count, :, n0 : n0 + CHUNK].rearrange("g j n -> j g n"),
+                    in_=y_last[half][:, g0 : g0 + count, :],
                 )
 
         nc.vector.memset(warm_in[:], 0.0)
@@ -221,8 +220,8 @@ def tile_rows_gnn_rgcn_kernel(tc, x, w1, ni1, ad1, w2, ni2, ad2, out):
         spread(2)
         round_w(1)
         spread(1)
-        quantize_w(1)
         spread(3)
+        quantize_w(1)
         for k in range(CHUNKS):
             for s in ROUNDS:
                 features(s, k)
@@ -255,9 +254,9 @@ def tile_rows_gnn_rgcn_kernel(tc, x, w1, ni1, ad1, w2, ni2, ad2, out):
         weigh_first(1, 1)
         quantize_h(0, 1, 1)
         edges(0, 1, 1, 0)
-        finish_last(0, 1, 0)
+        finish_last(0, 1, 0, 2)
         join_second(1, 1)
         for r in range(RELS):
             quantize_h(1, r, 1)
         edges(1, 1, 0, 2 * CHUNK)
-        finish_last(1, 0, 2 * CHUNK)
+        finish_last(1, 0, 2 * CHUNK, 1)

@@ -148,19 +148,18 @@ def tile_rows_gnn_rgcn_kernel(tc, x, w1, ni1, ad1, w2, ni2, ad2, out):
         def quantize_ad(r):
             quantize(ad_codes[r][:], ad_scales[r][:], ad_bf[r][:])
 
-        def edges(half, k, b, col):
-            for r in range(RELS):
-                c = 2 * half + r
-                for g in range(G):
-                    nc.tensor.matmul_mx(
-                        out=bank[g][b][:, col : col + CHUNK],
-                        lhsT=ad_codes[r][rows(g), :].bitcast(FP8X4),
-                        lhsT_scale=ad_scales[r][rows(g), :],
-                        rhs=h_codes[c][k][rows(g), :].bitcast(FP8X4),
-                        rhs_scale=h_scales[c][k][rows(g), :],
-                        start=(r == 0),
-                        stop=(r == RELS - 1),
-                    )
+        def edges(half, k, r, b, col, start, stop):
+            c = 2 * half + r
+            for g in range(G):
+                nc.tensor.matmul_mx(
+                    out=bank[g][b][:, col : col + CHUNK],
+                    lhsT=ad_codes[r][rows(g), :].bitcast(FP8X4),
+                    lhsT_scale=ad_scales[r][rows(g), :],
+                    rhs=h_codes[c][k][rows(g), :].bitcast(FP8X4),
+                    rhs_scale=h_scales[c][k][rows(g), :],
+                    start=start,
+                    stop=stop,
+                )
 
         def finish_last(half, b, col, count):
             n0 = first_column(half, 1)
@@ -228,22 +227,25 @@ def tile_rows_gnn_rgcn_kernel(tc, x, w1, ni1, ad1, w2, ni2, ad2, out):
 
         for half in range(2):
             weigh_second(half, 0)
-        interleave(nc.scalar.copy, ad_bf[0], ad_raw[0], 0, J)
+        interleave(nc.scalar.copy, ad_bf[1], ad_raw[1], 0, J)
         for half in range(2):
             weigh_second(half, 1)
 
         for half in range(2):
             weigh_first(half, 0)
+        interleave(nc.vector.tensor_copy, ad_bf[0], ad_raw[0], 0, J)
+        quantize_h(0, 0, 0)
+        quantize_ad(0)
+        quantize_h(1, 0, 0)
         for half in range(2):
-            quantize_h(half, 0, 0)
             join_second(half, 0)
-        interleave(nc.vector.tensor_copy, ad_bf[1], ad_raw[1], 0, J)
-        for half in range(2):
-            quantize_h(half, 1, 0)
-            quantize_ad(half)
+        quantize_h(0, 1, 0)
+        quantize_ad(1)
+        quantize_h(1, 1, 0)
 
-        for half in range(2):
-            edges(half, 0, 0, half * CHUNK)
+        for r in range(RELS):
+            for half in range(2):
+                edges(half, 0, r, 0, half * CHUNK, r == 0 and half == 0, r == RELS - 1 and half == 1)
         for g in range(G):
             nc.scalar.activation(out=y_first[g][:], in_=bank[g][0][:, 0 : 2 * CHUNK], func=ACT.Gelu_apprx_tanh)
             nc.sync.dma_start(out=out[g, :, 0 : 2 * CHUNK], in_=y_first[g][:])
@@ -253,10 +255,12 @@ def tile_rows_gnn_rgcn_kernel(tc, x, w1, ni1, ad1, w2, ni2, ad2, out):
         quantize_h(0, 0, 1)
         weigh_first(1, 1)
         quantize_h(0, 1, 1)
-        edges(0, 1, 1, 0)
+        for r in range(RELS):
+            edges(0, 1, r, 1, 0, r == 0, r == RELS - 1)
         finish_last(0, 1, 0, 2)
         join_second(1, 1)
         for r in range(RELS):
             quantize_h(1, r, 1)
-        edges(1, 1, 0, 2 * CHUNK)
+        for r in range(RELS):
+            edges(1, 1, r, 0, 2 * CHUNK, r == 0, r == RELS - 1)
         finish_last(1, 0, 2 * CHUNK, 1)

@@ -21,6 +21,7 @@ CHUNK = 128
 CHUNKS = 2
 GAP = P - R
 W_VECTOR_COLS = 88
+GRAPH_ORDER = ((2, 3, 0, 1), (0, 1, 2, 3))
 ROUNDS = (0, 2, 1, 3)
 
 
@@ -70,7 +71,7 @@ def tile_rows_gnn_rgcn_kernel(tc, x, w1, ni1, ad1, w2, ni2, ad2, out):
         ni = [sbuf("ni%d" % r, [P, PACK], F32) for r in range(RELS)]
         warm_in = sbuf("warm_in", [P, 8], F32)
         warm_out = sbuf("warm_out", [P, 8], F32)
-        h_places = [[sbuf("h_places%d_%d" % (half, k), [P, PACK, CHUNK], BF16) for k in range(CHUNKS)] for half in range(2)]
+        h_pairs = [sbuf("h_pairs%d" % k, [P, 2, CHUNK, 2], BF16) for k in range(CHUNKS)]
         h_bf = [[sbuf("h_bf%d_%d" % (c, k), [P, CHUNK, PACK], BF16) for k in range(CHUNKS)] for c in range(G)]
         h_codes = [[sbuf("h_codes%d_%d" % (c, k), [P, CHUNK], I32) for k in range(CHUNKS)] for c in range(G)]
         h_scales = [[sbuf("h_scales%d_%d" % (c, k), [P, CHUNK], U8) for k in range(CHUNKS)] for c in range(G)]
@@ -121,25 +122,28 @@ def tile_rows_gnn_rgcn_kernel(tc, x, w1, ni1, ad1, w2, ni2, ad2, out):
                         stop=(s == ROUNDS[-1] and t == PACK - 1),
                     )
 
-        def weigh_first(half, k):
+        def weigh(half, r, k):
             nc.vector.tensor_tensor(
-                out=h_bf[2 * half][k][:],
-                in0=bank[2 * half][k][:].rearrange("p (t n) -> p n t", t=PACK),
-                in1=ni[0][:].unsqueeze(1).to_broadcast([P, CHUNK, PACK]),
+                out=h_bf[2 * half + r][k][:],
+                in0=bank[2 * half + r][k][:].rearrange("p (t n) -> p n t", t=PACK),
+                in1=ni[r][:].unsqueeze(1).to_broadcast([P, CHUNK, PACK]),
                 op=ALU.mult,
             )
 
-        def weigh_second(half, k):
-            for t in range(PACK):
+        def weigh_places(k):
+            for t in (0, 2, 1, 3):
                 nc.scalar.activation(
-                    out=h_places[half][k][:, t, :],
-                    in_=bank[2 * half + 1][k][:, t * CHUNK : (t + 1) * CHUNK],
+                    out=h_pairs[k][:, t // 2, :, t % 2],
+                    in_=bank[1][k][:, t * CHUNK : (t + 1) * CHUNK],
                     func=ACT.Copy,
                     scale=ni[1][:, t : t + 1],
                 )
 
-        def join_second(half, k):
-            interleave(nc.vector.tensor_copy, h_bf[2 * half + 1][k], h_places[half][k], 0, CHUNK)
+        def join_pairs(k):
+            nc.vector.tensor_copy(
+                out=h_bf[1][k][:].rearrange("p n t -> p (n t)").bitcast(I32).rearrange("p (n u) -> p n u", u=2),
+                in_=h_pairs[k][:].rearrange("p u n e -> p (u n e)").bitcast(I32).rearrange("p (u n) -> p n u", u=2),
+            )
 
         def quantize_h(half, r, k):
             c = 2 * half + r
@@ -148,11 +152,18 @@ def tile_rows_gnn_rgcn_kernel(tc, x, w1, ni1, ad1, w2, ni2, ad2, out):
         def quantize_ad(r):
             quantize(ad_codes[r][:], ad_scales[r][:], ad_bf[r][:])
 
-        def edges(half, k, r, b, col, start, stop):
+        def y_sums(half, k, g):
+            if k == 0:
+                return bank[g][0][:, half * CHUNK : (half + 1) * CHUNK]
+            if (half == 0) == (g < 2):
+                return bank[g][1][:, 0:CHUNK]
+            return bank[g][0][:, 2 * CHUNK : 3 * CHUNK]
+
+        def edges(half, k, r, start, stop):
             c = 2 * half + r
-            for g in range(G):
+            for g in GRAPH_ORDER[k]:
                 nc.tensor.matmul_mx(
-                    out=bank[g][b][:, col : col + CHUNK],
+                    out=y_sums(half, k, g),
                     lhsT=ad_codes[r][rows(g), :].bitcast(FP8X4),
                     lhsT_scale=ad_scales[r][rows(g), :],
                     rhs=h_codes[c][k][rows(g), :].bitcast(FP8X4),
@@ -161,13 +172,12 @@ def tile_rows_gnn_rgcn_kernel(tc, x, w1, ni1, ad1, w2, ni2, ad2, out):
                     stop=stop,
                 )
 
-        def finish_last(half, b, col, count):
+        def finish_last(half, count):
             n0 = first_column(half, 1)
-            for g0 in range(0, G, count):
-                for g in range(g0, g0 + count):
-                    nc.scalar.activation(
-                        out=y_last[half][:, g, :], in_=bank[g][b][:, col : col + CHUNK], func=ACT.Gelu_apprx_tanh
-                    )
+            for i in range(0, G, count):
+                g0 = min(GRAPH_ORDER[1][i : i + count])
+                for g in GRAPH_ORDER[1][i : i + count]:
+                    nc.scalar.activation(out=y_last[half][:, g, :], in_=y_sums(half, 1, g), func=ACT.Gelu_apprx_tanh)
                 nc.sync.dma_start(
                     out=out[g0 : g0 + count, :, n0 : n0 + CHUNK].rearrange("g j n -> j g n"),
                     in_=y_last[half][:, g0 : g0 + count, :],
@@ -225,42 +235,40 @@ def tile_rows_gnn_rgcn_kernel(tc, x, w1, ni1, ad1, w2, ni2, ad2, out):
             for s in ROUNDS:
                 features(s, k)
 
-        for half in range(2):
-            weigh_second(half, 0)
-        interleave(nc.scalar.copy, ad_bf[1], ad_raw[1], 0, J)
-        for half in range(2):
-            weigh_second(half, 1)
+        weigh_places(0)
+        for r in range(RELS):
+            interleave(nc.scalar.copy, ad_bf[r], ad_raw[r], 0, J)
+        weigh_places(1)
 
-        for half in range(2):
-            weigh_first(half, 0)
-        interleave(nc.vector.tensor_copy, ad_bf[0], ad_raw[0], 0, J)
+        weigh(0, 0, 0)
+        for r in range(RELS):
+            weigh(1, r, 0)
         quantize_h(0, 0, 0)
-        quantize_ad(0)
+        join_pairs(0)
         quantize_h(1, 0, 0)
-        for half in range(2):
-            join_second(half, 0)
-        quantize_h(0, 1, 0)
+        quantize_ad(0)
+        for half in (1, 0):
+            quantize_h(half, 1, 0)
         quantize_ad(1)
-        quantize_h(1, 1, 0)
 
         for r in range(RELS):
             for half in range(2):
-                edges(half, 0, r, 0, half * CHUNK, r == 0 and half == 0, r == RELS - 1 and half == 1)
-        for g in range(G):
+                edges(half, 0, r, r == 0 and half == 0, r == RELS - 1 and half == 1)
+        for g in GRAPH_ORDER[0]:
             nc.scalar.activation(out=y_first[g][:], in_=bank[g][0][:, 0 : 2 * CHUNK], func=ACT.Gelu_apprx_tanh)
             nc.sync.dma_start(out=out[g, :, 0 : 2 * CHUNK], in_=y_first[g][:])
 
-        weigh_first(0, 1)
-        join_second(0, 1)
-        quantize_h(0, 0, 1)
-        weigh_first(1, 1)
-        quantize_h(0, 1, 1)
+        for half in range(2):
+            weigh(half, 0, 1)
+        join_pairs(1)
         for r in range(RELS):
-            edges(0, 1, r, 1, 0, r == 0, r == RELS - 1)
-        finish_last(0, 1, 0, 2)
-        join_second(1, 1)
+            quantize_h(0, r, 1)
+        for r in range(RELS):
+            edges(0, 1, r, r == 0, r == 1)
+        finish_last(0, 2)
+        weigh(1, 1, 1)
         for r in range(RELS):
             quantize_h(1, r, 1)
         for r in range(RELS):
-            edges(1, 1, r, 0, 2 * CHUNK, r == 0, r == RELS - 1)
-        finish_last(1, 0, 2 * CHUNK, 1)
+            edges(1, 1, r, r == 0, r == 1)
+        finish_last(1, 1)

from contextlib import ExitStack

import concourse.mybir as mybir

G, D, I, N, J = 4, 128, 128, 512, 128
FLOPS = 2 * 2 * G * I * D * N + 2 * 2 * G * J * I * N

F32 = mybir.dt.float32
BF16 = mybir.dt.bfloat16
I32 = mybir.dt.int32
U8 = mybir.dt.uint8
FP8X4 = mybir.dt.float8_e4m3fn_x4
ACT = mybir.ActivationFunctionType
ALU = mybir.AluOpType

P = 128
R = 32
PACK = 4
RELS = 2
CHUNK = 128
CHUNKS = 2
GAP = P - R
W_VECTOR_COLS = 88
GRAPH_ORDER = ((2, 3, 0, 1), (0, 1, 2, 3))
ROUNDS = (0, 2, 1, 3)


def interleave(copy, dst, src, c0, c1):
    copy(
        out=dst[:, c0:c1, :].rearrange("p (c i) t -> p c t i", i=4),
        in_=src[:, :, c0:c1].rearrange("p t (c i) -> p c t i", i=4),
    )


def tile_rows_gnn_rgcn_kernel(tc, x, w1, ni1, ad1, w2, ni2, ad2, out):
    nc = tc.nc
    ws, nis, ads = (w1, w2), (ni1, ni2), (ad1, ad2)

    def rows(tile, count=1):
        return slice(R * tile, R * (tile + count))

    def first_column(half, k):
        return k * 2 * CHUNK + half * CHUNK

    def quantize(codes, scales, src):
        nc.vector.quantize_mx(out=codes.bitcast(FP8X4), scales=scales, in_=src.rearrange("p c t -> p (c t)"))

    with ExitStack() as ctx:
        sb = ctx.enter_context(tc.tile_pool(name="sb", bufs=1))
        ps = ctx.enter_context(tc.psum_pool(name="ps", bufs=1))
        ctx.enter_context(tc.manual_schedule())

        def sbuf(name, shape, dtype):
            return sb.tile(shape, dtype, name=name, align_bytes=64)

        bank = [[ps.tile([P, N], F32, name="bank%d_%d" % (c, k)) for k in range(CHUNKS)] for c in range(G)]

        w_raw = [sbuf("w_raw%d" % k, [P, PACK, CHUNK], F32) for k in range(CHUNKS)]
        w_bf = [sbuf("w_bf%d" % k, [P, CHUNK, PACK], BF16) for k in range(CHUNKS)]
        w_codes = [sbuf("w_codes%d" % k, [P, CHUNK], I32) for k in range(CHUNKS)]
        w_scales = [sbuf("w_scales%d" % k, [P, CHUNK], U8) for k in range(CHUNKS)]
        x_raw = sbuf("x_raw", [P, PACK, I], F32)
        x_bf = sbuf("x_bf", [P, I, PACK], BF16)
        x_mx = [sbuf("x_mx%d" % s, [P, I + I // 4], I32) for s in range(G)]
        x_pad = [sbuf("x_pad%d" % s, [P, GAP + PACK * P], I32) for s in range(G)]
        x_scales = [sbuf("x_scales%d" % s, [P, PACK, P], U8) for s in range(G)]
        ad_raw = [sbuf("ad_raw%d" % r, [P, PACK, J], F32) for r in range(RELS)]
        ad_bf = [sbuf("ad_bf%d" % r, [P, J, PACK], BF16) for r in range(RELS)]
        ad_codes = [sbuf("ad_codes%d" % r, [P, J], I32) for r in range(RELS)]
        ad_scales = [sbuf("ad_scales%d" % r, [P, J], U8) for r in range(RELS)]
        ni = [sbuf("ni%d" % r, [P, PACK], F32) for r in range(RELS)]
        warm_in = sbuf("warm_in", [P, 8], F32)
        warm_out = sbuf("warm_out", [P, 8], F32)
        h_pairs = [sbuf("h_pairs%d" % k, [P, 2, CHUNK, 2], BF16) for k in range(CHUNKS)]
        h_bf = [[sbuf("h_bf%d_%d" % (c, k), [P, CHUNK, PACK], BF16) for k in range(CHUNKS)] for c in range(G)]
        h_codes = [[sbuf("h_codes%d_%d" % (c, k), [P, CHUNK], I32) for k in range(CHUNKS)] for c in range(G)]
        h_scales = [[sbuf("h_scales%d_%d" % (c, k), [P, CHUNK], U8) for k in range(CHUNKS)] for c in range(G)]
        y_first = [sbuf("y_first%d" % g, [P, 2 * CHUNK], F32) for g in range(G)]
        y_last = [sbuf("y_last%d" % half, [P, G, CHUNK], F32) for half in range(2)]

        def load_w(queue, c, k):
            n0 = first_column(c // RELS, k)
            queue.dma_start(
                out=w_raw[k][rows(c), :, :], in_=ws[c % RELS][:, n0 : n0 + CHUNK].rearrange("(p t) n -> p t n", t=PACK)
            )

        def round_w(k):
            interleave(nc.vector.tensor_copy, w_bf[k], w_raw[k], 0, W_VECTOR_COLS)
            interleave(nc.scalar.copy, w_bf[k], w_raw[k], W_VECTOR_COLS, CHUNK)

        def quantize_w(k):
            quantize(w_codes[k][:], w_scales[k][:], w_bf[k][:])

        def zero_gaps(s):
            nc.vector.memset(x_pad[s][:, 0:GAP], 0)
            nc.vector.memset(x_pad[s][:, GAP:].rearrange("p (t m) -> p t m", m=P)[:, :, R:P], 0)

        def hand_on(queue, s, src, count):
            queue.dma_start(out=x_mx[s][rows((src + s) % G, count), :], in_=x_mx[0][rows(src, count), :])

        def spread(s):
            nc.vector.tensor_copy(
                out=x_pad[s][:, GAP:].rearrange("p (t m) -> p t m", m=P)[:, :, 0:R],
                in_=x_mx[s][:, 0:I].rearrange("p (t m) -> p t m", m=R),
            )
            nc.vector.tensor_copy(
                out=x_scales[s][:].bitcast(I32).rearrange("p t (g b) -> p t g b", g=G),
                in_=x_mx[s][:, I:].rearrange("p (t b) -> p t b", t=PACK).unsqueeze(2).to_broadcast([P, PACK, G, R // 4]),
            )

        def features(s, k):
            for t in range(PACK):
                for c in range(G):
                    word0 = GAP + P * t - R * ((c - s) % G)
                    nc.tensor.matmul_mx(
                        out=bank[c][k][:, t * CHUNK : (t + 1) * CHUNK],
                        lhsT=x_pad[s][rows(c), word0 : word0 + P].bitcast(FP8X4),
                        lhsT_scale=x_scales[s][rows(c), t, :],
                        rhs=w_codes[k][rows(c), :].bitcast(FP8X4),
                        rhs_scale=w_scales[k][rows(c), :],
                        start=(s == ROUNDS[0] and t == 0),
                        stop=(s == ROUNDS[-1] and t == PACK - 1),
                    )

        def weigh(half, r, k):
            nc.vector.tensor_tensor(
                out=h_bf[2 * half + r][k][:],
                in0=bank[2 * half + r][k][:].rearrange("p (t n) -> p n t", t=PACK),
                in1=ni[r][:].unsqueeze(1).to_broadcast([P, CHUNK, PACK]),
                op=ALU.mult,
            )

        def weigh_places(k):
            for t in (0, 2, 1, 3):
                nc.scalar.activation(
                    out=h_pairs[k][:, t // 2, :, t % 2],
                    in_=bank[1][k][:, t * CHUNK : (t + 1) * CHUNK],
                    func=ACT.Copy,
                    scale=ni[1][:, t : t + 1],
                )

        def join_pairs(k):
            nc.vector.tensor_copy(
                out=h_bf[1][k][:].rearrange("p n t -> p (n t)").bitcast(I32).rearrange("p (n u) -> p n u", u=2),
                in_=h_pairs[k][:].rearrange("p u n e -> p (u n e)").bitcast(I32).rearrange("p (u n) -> p n u", u=2),
            )

        def quantize_h(half, r, k):
            c = 2 * half + r
            quantize(h_codes[c][k][:], h_scales[c][k][:], h_bf[c][k][:])

        def quantize_ad(r):
            quantize(ad_codes[r][:], ad_scales[r][:], ad_bf[r][:])

        def y_sums(half, k, g):
            if k == 0:
                return bank[g][0][:, half * CHUNK : (half + 1) * CHUNK]
            if (half == 0) == (g < 2):
                return bank[g][1][:, 0:CHUNK]
            return bank[g][0][:, 2 * CHUNK : 3 * CHUNK]

        def edges(half, k, r, start, stop):
            c = 2 * half + r
            for g in GRAPH_ORDER[k]:
                nc.tensor.matmul_mx(
                    out=y_sums(half, k, g),
                    lhsT=ad_codes[r][rows(g), :].bitcast(FP8X4),
                    lhsT_scale=ad_scales[r][rows(g), :],
                    rhs=h_codes[c][k][rows(g), :].bitcast(FP8X4),
                    rhs_scale=h_scales[c][k][rows(g), :],
                    start=start,
                    stop=stop,
                )

        def finish_last(half, count):
            n0 = first_column(half, 1)
            for i in range(0, G, count):
                g0 = min(GRAPH_ORDER[1][i : i + count])
                for g in GRAPH_ORDER[1][i : i + count]:
                    nc.scalar.activation(out=y_last[half][:, g, :], in_=y_sums(half, 1, g), func=ACT.Gelu_apprx_tanh)
                nc.sync.dma_start(
                    out=out[g0 : g0 + count, :, n0 : n0 + CHUNK].rearrange("g j n -> j g n"),
                    in_=y_last[half][:, g0 : g0 + count, :],
                )

        nc.vector.memset(warm_in[:], 0.0)
        nc.vector.memset(x_mx[0][:, I:], 0)
        for s in ROUNDS[:3]:
            zero_gaps(s)

        x_rows = x.rearrange("g (p t) i -> (g p) t i", t=PACK)
        nc.sync.dma_start(out=x_raw[:, 0:2, :], in_=x_rows[:, 0:2, :])
        nc.scalar.dma_start(out=x_raw[:, 2:4, :], in_=x_rows[:, 2:4, :])
        for k in range(CHUNKS):
            load_w(nc.sync, 0, k)
            load_w(nc.scalar, 2, k)
            load_w(nc.sync, 1, k)
            if k == 0:
                load_w(nc.scalar, 3, k)
        nc.scalar.activation(out=warm_out[:], in_=warm_in[:], func=ACT.Gelu_apprx_tanh)

        for u, copy in enumerate((nc.vector.tensor_copy, nc.scalar.copy)):
            copy(
                out=x_bf[:].rearrange("p (t m) j -> p m t j", t=PACK)[:, :, 2 * u : 2 * u + 2],
                in_=x_raw[:].rearrange("p j (m t) -> p m t j", t=PACK)[:, :, 2 * u : 2 * u + 2],
            )
        load_w(nc.scalar, 3, 1)
        for u in range(2):
            cols = slice(u * I // 2, (u + 1) * I // 2)
            quantize(x_mx[0][:, cols], x_mx[0][:, I:].bitcast(U8)[:, cols], x_bf[:, cols, :])

        hand_on(nc.sync, 2, 2, 2)
        hand_on(nc.scalar, 2, 0, 2)
        spread(0)
        round_w(0)
        quantize_w(0)
        hand_on(nc.sync, 1, 0, 2)
        hand_on(nc.scalar, 1, 2, 1)
        hand_on(nc.sync, 1, 3, 1)
        hand_on(nc.scalar, 3, 3, 1)
        hand_on(nc.sync, 3, 1, 2)
        hand_on(nc.sync, 3, 0, 1)
        for r in range(RELS):
            nc.sync.dma_start(out=ni[r][:], in_=nis[r].rearrange("g (p t) o -> (g p) (t o)", t=PACK))
        for r in range(RELS):
            nc.sync.dma_start(out=ad_raw[r][:], in_=ads[r].rearrange("g (p t) j -> (g p) t j", t=PACK))

        zero_gaps(3)
        spread(2)
        round_w(1)
        spread(1)
        spread(3)
        quantize_w(1)
        for k in range(CHUNKS):
            for s in ROUNDS:
                features(s, k)

        weigh_places(0)
        for r in range(RELS):
            interleave(nc.scalar.copy, ad_bf[r], ad_raw[r], 0, J)
        weigh_places(1)

        weigh(0, 0, 0)
        for r in range(RELS):
            weigh(1, r, 0)
        quantize_h(0, 0, 0)
        join_pairs(0)
        quantize_h(1, 0, 0)
        quantize_ad(0)
        for half in (1, 0):
            quantize_h(half, 1, 0)
        quantize_ad(1)

        for r in range(RELS):
            for half in range(2):
                edges(half, 0, r, r == 0 and half == 0, r == RELS - 1 and half == 1)
        for g in GRAPH_ORDER[0]:
            nc.scalar.activation(out=y_first[g][:], in_=bank[g][0][:, 0 : 2 * CHUNK], func=ACT.Gelu_apprx_tanh)
            nc.sync.dma_start(out=out[g, :, 0 : 2 * CHUNK], in_=y_first[g][:])

        for half in range(2):
            weigh(half, 0, 1)
        join_pairs(1)
        for r in range(RELS):
            quantize_h(0, r, 1)
        for r in range(RELS):
            edges(0, 1, r, r == 0, r == 1)
        finish_last(0, 2)
        weigh(1, 1, 1)
        for r in range(RELS):
            quantize_h(1, r, 1)
        for r in range(RELS):
            edges(1, 1, r, r == 0, r == 1)
        finish_last(1, 1)
